import numpy as np, ml_dtypes
CORES = [3,11,19,27,35,43,51,59]
N = 8
BF = ml_dtypes.bfloat16
V, M, CAP, RO = 512, 1, 32, 2
def phone(rng):
    loc = rng.choice(np.array([0.0, 0.2, 0.5, 0.8]), (N, 8, 1, 1))
    far = rng.integers(0, N * V, (N, 8, 16, V)); near = rng.integers(0, V, (N, 8, 16, V)) + V * np.arange(N)[:, None, None, None]
    return np.where(rng.random((N, 8, 16, V)) < loc, near, far)
def lore(rng):
    share = rng.choice(np.array([0.0, 0.0, 0.0625, 0.125, 0.3]), (N, 8, 1, V))
    return np.where(rng.random((N, 8, 16, V)) < share, rng.integers(1, 256, (N, 8, 16, V)), 0)
def dense(rng, sec, tel, g, d, lean):
    x = np.arange(N * V).reshape(N, 1, V); goal = x[:, 0] ^ 1; h = V // 2; i = 0
    run = 2 * ((64 * int(rng.integers(0, V // 128)) + rng.permutation((N - 1) * CAP)) % h)
    for r in range(N):
        if r == d: continue
        goal[r, 2 * rng.permutation(h)[:CAP]] = d * V + run[i:i + CAP]; i += CAP
    s = rng.integers(0, 256, (N, 16, V)); a, b = (int(k) for k in rng.permutation(16)[:2])
    s[:, a, 0::2] = rng.integers(0, 51, (N, h)); s[d, a, 0::2] = rng.integers(51, 101, h); s[:, a, 1::2] = rng.integers(101, 256, (N, h))
    s[:, b, 0::2] = rng.integers(128, 256, (N, h)); s[:, b, 1::2] = rng.integers(0, 128, (N, h))
    sec[:, g] = s
    if lean:
        row = rng.integers(0, 16, (N, 1, V)); t = np.where(np.arange(16)[None, :, None] == row, goal[:, None, :], x)
        if M == 2: t[:, :, 1::2] = tel[:, g, :, 1::2]
        tel[:, g] = t
    else: tel[:, g] = goal[:, None, :]
def pack(sec, tel):
    return {"sec": np.ascontiguousarray(sec.reshape(N, 128, V)).astype(np.float32).astype(BF), "tel": np.ascontiguousarray(tel.reshape(N, 128, V)).astype(np.int32)}
def setup_inputs(rng):
    tel, sec = phone(rng), lore(rng); me = np.arange(N * V).reshape(N, 1, 1, V)
    tel = np.where(rng.random((N, 8, 1, V)) < 0.03, me, tel); sec = np.where(rng.random((N, 8, 1, V)) < 0.004, 255, sec)
    return pack(sec, tel)
def setup_inputs_room(rng):
    b = rng.integers(0, 100, (8, 16)); sec = np.broadcast_to(b[None, :, :, None], (N, 8, 16, V)).copy()
    o = np.argsort(rng.random((N, 8, V)), axis=-1); kn, non = o[:, :, :16], o[:, :, 16:]
    s = rng.integers(0, N, (N, 8, 16, V)); tel = s * V + non[s, np.arange(8)[None, :, None, None], rng.integers(0, V - 16, (N, 8, 16, V))]
    for q in range(N):
        for g in range(8):
            sec[q, g][:, kn[q, g]] = b[g][:, None] + rng.integers(1, 100, (16, 16))
            cal = non[q, g][non[q, g] % M == 0]; pos = 0
            for d in range(1, N + 1):
                z = (q + d) % N; n = int(rng.choice(np.array([0, 1, CAP - 1, CAP, CAP + 1, CAP + 8])))
                if q == 0 and d == 1: n = (CAP, CAP + 1, CAP - 1, CAP + 8, 1, 0, CAP, CAP + 1)[g]
                if d == N: n = 20
                tel[q, g, rng.integers(0, 16, n), cal[pos:pos + n]] = z * V + kn[z, g, rng.integers(0, 16, n)]
                pos += n
    return pack(sec, tel)
def setup_inputs_ties(rng):
    tel = phone(rng); tel[:, :, 8:] = tel[:, :, 7::-1]
    sec = (rng.random((N, 8, 16, V)) < rng.choice(np.array([0.05, 0.2, 0.5]), (N, 8, 1, V))).astype(np.int64)
    sec[:, ::2] *= 255
    m = rng.random((N, 4, 16, V)) < 0.1
    tel[:, 1::2] = np.where(m, rng.choice(np.array([0, V - 1, V, N * V - 1]), m.shape), tel[:, 1::2])
    return pack(sec, tel)
def setup_inputs_crowd(rng):
    tel, sec = phone(rng), lore(rng); x = np.arange(N * V).reshape(N, 1, V); o = rng.permutation(8)
    for g in o[:3]: sec[:, g] = rng.integers(0, 256, (N, 16, V))
    tel[:, o[0]] = (x + M) % (N * V); tel[:, o[1]] = x ^ M; tel[:, o[2]] = (x + V) % (N * V)
    sec[:, o[3:5]] = np.minimum(sec[:, o[3:5]], 200)
    star = int(rng.choice(np.array([0, V - 1, N * V - V, N * V - 1]))); tel[:, o[3], int(rng.integers(0, 16))] = star; sec[star // V, o[3], :, star % V] = 255
    place = rng.choice(np.array([0, V - 1]), N)
    tel[:, o[4], int(rng.integers(0, 16))] = (np.arange(N) * V + place)[rng.integers(0, N, (N, V))]
    for q in range(N): sec[q, o[4], :, place[q]] = 255
    dense(rng, sec, tel, int(o[5]), N - 1, False)
    dense(rng, sec, tel, int(o[6]), int(rng.integers(0, N - 1)), True)
    return pack(sec, tel)
def setup_inputs_alike(rng):
    tel, sec = phone(rng), lore(rng); x = np.arange(N * V).reshape(N, 1, V); o = rng.permutation(8)
    sec[:, o[0]] = rng.integers(0, 256, (1, 16, 1))
    sec[:, o[1]] = 0; sec[int(rng.integers(0, N)), o[1]] = 255
    one = int(rng.choice(np.array([0, N * V - 1]))); sec[:, o[2]] = 0; sec[one // V, o[2], int(rng.integers(0, 16)), one % V] = int(rng.integers(1, 256)); tel[:, o[2], 15] = one
    tel[:, o[3], 1:] = x
    sec[:, o[4]] = rng.integers(254, 256, (N, 16, V))
    sec[:, o[5]] = np.where(rng.random((N, 1, V)) < 0.5, 0, rng.integers(230, 256, (N, 16, V)))
    z = rng.integers(-40, 41, (N, 8, V)); s = 128 + np.concatenate([z, -z], axis=1); s[:, int(rng.integers(0, 16))] += rng.integers(-1, 2, (N, V))
    sec[:, o[6]] = np.where(rng.random((N, 1, V)) < 0.5, 0, s)
    return pack(sec, tel)
def setup_inputs_spread(rng):
    sec = np.floor(np.exp2(8 * rng.random((N, 8, 1, V))) * np.exp2(-4 * rng.random((1, 8, 16, 1))) * rng.random((N, 8, 16, V))).astype(np.int64)
    sec = np.where(rng.random((N, 8, 16, V)) < rng.random((N, 8, 1, V)), np.minimum(sec, 255), 0)
    o = np.argsort(rng.random((8, N * V)), axis=-1); k = np.minimum((N * V * rng.random((N, 8, 16, V)) ** 3).astype(np.int64), N * V - 1)
    return pack(sec, o[np.arange(8)[None, :, None, None], k])
def check_inputs(d):
    bad = []; s = np.asarray(d["sec"]).astype(np.float32); a = np.asarray(d["tel"])
    if not np.all((s >= 0) & (s <= 255) & (s == np.floor(s))): bad.append("sec: whole numbers from 0 to 255")
    if np.min(a) < 0 or np.max(a) > N * V - 1: bad.append("range of tel")
    return bad
def world(a):
    return np.ascontiguousarray(a.astype(np.int64).reshape(N, 8, 16, V).transpose(1, 2, 0, 3)).reshape(8, 16, N * V)
def ranks(a):
    return np.ascontiguousarray(a.reshape(8, 16, N, V).transpose(2, 0, 1, 3)).reshape(N, 128, V).astype(np.float32)
def reference(sec, tel):
    S, T = world(sec.astype(np.float32)), world(tel)
    for t in range(RO):
        x = (np.arange(N)[:, None] * V + np.arange(t % M, V, M)[None, :]).reshape(-1)
        Sn, Tn = S.copy(), T.copy()
        for g in range(8):
            tl = T[g][:, x]; gain = np.zeros(tl.shape, np.int64)
            for f in range(16): gain += np.maximum(S[g, f][tl] - S[g, f][x][None, :], 0)
            row = np.argmax(gain, axis=0)
            c = np.take_along_axis(tl, row[None, :], 0)[0]; call = np.max(gain, axis=0) > 0
            through = call.reshape(N, -1)
            for s in range(N):
                flag = (call & (c // V == s)).reshape(N, -1); count = np.add.accumulate(flag.astype(np.int64), axis=1)
                through = through & (~flag | (count <= CAP) | (np.arange(N)[:, None] == s))
            w = np.flatnonzero(through.reshape(-1)); u, first = np.unique(c[w], return_index=True); w = w[first]; v = x[w]
            Sn[g][:, v] = np.maximum(S[g][:, v], S[g][:, u])
            Sn[g][:, u] = np.maximum(Sn[g][:, u], S[g][:, v])
            Tn[g][:, v] = np.where(gain[:, w] == 0, T[g][:, u], T[g][:, v])
            Tn[g, t, u] = v
        S, T = Sn, Tn
        if t < RO - 1: T = np.roll(Tn, 1, axis=0)
    return {"ysec": ranks(S).astype(BF), "ytel": ranks(T)}

@@ -1,0 +1,503 @@
+import math
+from concourse.bass import DstId, RemoteDMATransfer
+from concourse.mybir import AluOpType, ActivationFunctionType
+
+A = AluOpType
+F = ActivationFunctionType
+N = 8
+BIG = float(2 ** 23)
+MAGIC = 1.5 * 2 ** 29
+BASE = 2.2
+LAM = math.log(BASE)
+NV = 5
+
+SCRATCH = {}
+for _d, _s in (("bfloat16", "dsec lsec dS oS"), ("float16", "dtel ltel")):
+    for _k in _s.split():
+        SCRATCH[_k] = ("dram", [8, 128, 64], _d)
+for _k in ("dT0", "dT1", "oT0", "oT1"):
+    SCRATCH[_k] = ("dram", [8, 128, 32], "float32")
+for _d, _s in (
+        ("bfloat16", "own0:512 own1:512 own2:512 W:4096 OW:%d MX:8192 GS:%d OT:256 HH:512 OH:256 DH:512 HA:1024 BB:4096 "
+                     "Z:1024 ZS:512 IX:1024 HAS2:32 EQ:512 NZ:512 SA:512 ZH:512 "
+                     "IO:256 IOF:128 IOQ:128 EXP:2048 OI:256 ROWS:256 BROW:128 KROW:128 ONES:512 R2K:128 ID:128 IDN:128 "
+                     "IDB:128 ES:1024 BL:144 BON:128 B8:8 XB:144 SB0:240 XR:2304 BT:288 IM:256 P1M:128 SH:256 TRI:128 "
+                     "TR0:128 SB:1920" % (1024 * NV, 1024 * (8 - NV))),
+        ("float16", "ST16:512 t0:512 t1:512 TN:512 C16:32 WT16:32 NEW:32"),
+        ("float32", "TO:512 TT:4096 TF:512 DD:1024 SC:1024 NC:32 U1:32 X1:32 S16:32 PU:32 EM:256 WT:32 XL:64 LL:64 N128:32 "
+                    "AA:32 AB:32 Y:32 WN:32 CL:32 TX:32 D1:32 DX:32 WN2:256 E1:32 C2:32 EE:512 GT:512 "
+                    "PF:16 NR:512 SELF:32 SELF16:32 SELFK:32 MB:16 MC:8 DE:256 WC:8"),
+        ("int32", "ST:512 TI:64 AI:64 CM:32 SI:32 LO:32 AU:32 KI:32 CX:32 CI:32 PI:8"),
+        ("uint16", "U:512 CU:32 IDX:32 C2U:32")):
+    for _k in _s.split():
+        SCRATCH[_k.split(":")[0]] = ("sbuf", [128, int(_k.split(":")[1])], _d)
+for _k in range(8):
+    SCRATCH["P%d" % _k] = ("psum", [128, 512], "float32")
+
+SEMAPHORES = (["cv", "cs", "cp", "cg", "ls", "asec", "atel", "ah0", "ah1", "aT0", "aT1", "aS"]
+              + ["d%d" % _k for _k in range(22)])
+
+
+def rank_program(g, core, T, topo):
+    w = T.rank_of(core)
+    if w is None:
+        return
+    cores = list(T.cores)
+    Q = {"v": g.vector, "s": g.scalar, "p": g.tensor, "g": g, "y": g.sync}
+    cnt = {"cv": 0, "cs": 0, "cp": 0, "cg": 0}
+    seen = {e: {} for e in Q}
+    wr, rd, total, nd = {}, {}, {}, [0]
+    names = {T[k].name: k for k in SCRATCH}
+
+    def need(e, R, W):
+        toks = []
+        for k in R:
+            if k in wr:
+                toks.append(wr[k])
+            if k[0] == "P" and k[1:].isdigit():
+                toks += [t for t in rd.get(k, []) if t[2] != e]
+        for k in W:
+            toks += [t for t in rd.get(k, []) + ([wr[k]] if k in wr else []) if t[2] != e or e != "p"]
+        top = {}
+        for s, v, _e in toks:
+            top[s] = max(top.get(s, 0), v)
+        for s, v in top.items():
+            if seen[e].get(s, 0) < v:
+                Q[e].wait_ge(T.sem[s], v)
+                seen[e][s] = v
+
+    def mark(tok, R, W):
+        for k in R:
+            rd.setdefault(k, []).append(tok)
+        for k in W:
+            wr[k] = tok
+            rd[k] = []
+
+    def op(e, fn, R, W):
+        need(e, R, W)
+        s = "c" + e
+        cnt[s] += 1
+        fn().then_inc(T.sem[s], 1)
+        mark((s, cnt[s], e), R, W)
+
+    def dma(items):
+        s = "d%d" % nd[0]
+        nd[0] += 1
+        for e, o, i, R, W in items:
+            need(e, R, W)
+            Q[e].dma_start(o, i).then_inc(T.sem[s], 16)
+        total[s] = 16 * len(items)
+        for e, o, i, R, W in items:
+            mark((s, total[s], "d"), R, W)
+
+    def nm(ap):
+        return names[ap.name]
+
+    def cols(*xs):
+        return [nm(s) for s in xs if s is not None and not isinstance(s, (int, float))]
+
+    def ts(o, i, s1, s2, o0, o1=None, R=None, W=None):
+        r = (list(R) if R else [nm(i)]) + cols(s1, s2)
+        if o1 is None:
+            op("v", lambda: g.vector.tensor_scalar(o, i, s1, None, o0), r, W or [nm(o)])
+        else:
+            op("v", lambda: g.vector.tensor_scalar(o, i, s1, s2, o0, o1), r, W or [nm(o)])
+
+    def tt(o, a, b, o0, R=None, W=None):
+        op("v", lambda: g.vector.tensor_tensor(o, a, b, o0), R or [nm(a), nm(b)], W or [nm(o)])
+
+    def cp(o, i, R=None, W=None):
+        op("v", lambda: g.vector.tensor_copy(o, i), R or [nm(i)], W or [nm(o)])
+
+    def ms(o, c, W=None):
+        op("v", lambda: g.vector.memset(o, c), [], W or [nm(o)])
+
+    def scan(o, d0, d1, init, o0, o1, R=None, W=None):
+        op("v", lambda: g.vector.tensor_tensor_scan(o, d0, d1, init, o0, o1), R or [nm(d0), nm(d1)], W or [nm(o)])
+
+    def act(o, i, f, bias=0.0, scale=1.0, R=None, W=None):
+        r = (list(R) if R else [nm(i)]) + cols(bias, scale)
+        op("s", lambda: g.scalar.activation(o, i, f, bias=bias, scale=scale), r, W or [nm(o)])
+
+    def mm(o, l, r, a=True, z=True, R=None):
+        op("p", lambda: g.tensor.matmul(o, l, r, a, z), R or [nm(l), nm(r)], [nm(o)])
+
+    def iota(o, pat, base, ch):
+        if nm(o) == "PI":
+            op("g", lambda: g.iota(o, pat, base, ch), [], [nm(o)])
+        else:
+            op("g", lambda: g.iota(o, pat, base, ch, allow_small_or_imprecise_dtypes=True), [], [nm(o)])
+
+    sent = [0]
+
+    def spread(src, dst, sem, R):
+        need("g", R, [])
+        tr = []
+        for k in range(1, N):
+            r = (w + k) % N
+            rid, pid, _se = topo.addr(cores[r])
+            tr.append(RemoteDMATransfer(dst_ids=[DstId(rid=rid, pnc=pid)],
+                                        dma_engine_mask=1 << topo.engines(core, cores[r])[k - 1],
+                                        remote_sem=T.sem[sem], src=src[r], dst=dst))
+        g.remote_dma_fused(tr, local_sem=T.sem.ls)
+        sent[0] += N - 1
+        total[sem] = N - 1
+
+    P = [T["P%d" % k] for k in range(8)]
+    rows = slice(16 * w, 16 * w + 16)
+    half = [slice(0, 256), slice(256, 512)]
+
+    dma([("y", T.dsec[:], T.sec[:], [], ["dsec"])])
+    dma([("s", T.ST[:], T.tel[:], [], ["ST"])])
+    dma([("y", T.lsec[w], T.sec[rows, :], [], ["lsecw"])])
+    iota(T.IO[:], [[1, 256]], 0, 0)
+    iota(T.PI[:, 0:1], [[1, 1]], 0, 1)
+    iota(T.IOF[:], [[0, 8], [1, 16]], 0, 0)
+    iota(T.IOQ[:], [[1, 8], [0, 16]], 0, 0)
+    spread(T.dsec, T.lsec[w], "asec", ["dsec"])
+
+    pc, qc, bc = T.PF[:, 0:1], T.PF[:, 1:2], T.PF[:, 2:3]
+    ms(T.ONES[:], 1.0)
+    ms(T.DD[:, 0:512], 0.0, W=["DD0"])
+    ms(T.DE[:], 0.0)
+    ts(T.PI[:, 1:2], T.PI[:, 0:1], 4, None, A.arith_shift_right, R=["PI"], W=["PI1"])
+    ts(T.PI[:, 2:3], T.PI[:, 0:1], 15, None, A.bitwise_and, R=["PI"], W=["PI2"])
+    cp(T.PF[:, 0:3], T.PI[:, 0:3], R=["PI", "PI1", "PI2"])
+    for s in range(8):
+        ts(T.ES[:, 128 * s:128 * s + 128], T.IOF[:], float(16 * s), pc, A.add, A.is_equal, W=["ES%d" % s])
+    ts(T.ST16[:], T.ST[:], -2048.0, None, A.add)
+    dma([("s", T.dtel[:], T.ST16[:], ["ST16"], ["dtel"])])
+    dma([("y", T.ltel[w], T.ST16[rows, :], ["ST16"], ["ltelw"])])
+    iota(T.OI[:], [[0, 4], [1, 8], [-1, 8]], 0, 0)
+    iota(T.SELF16[:], [[16, 32]], -2048, 0)
+    iota(T.NR[:], [[1, 512]], -2048, 0)
+    spread(T.dtel, T.ltel[w], "atel", ["dtel"])
+    wr["lsec"] = ("asec", N - 1, "r")
+    wr["ltel"] = ("atel", N - 1, "r")
+    dma([("y", T.own0[:], T.lsec[:], ["lsec", "lsecw"], ["own0"])])
+    dma([("y", T.t0[:], T.ltel[:], ["ltel", "ltelw"], ["t00", "t01"])])
+
+    for c in (0, 1, 2, 3):
+        op("g", lambda: g.affine_select(T.EXP[:, 512 * c:512 * c + 512], T.ONES[:], [[1, 32], [0, 16]], A.is_equal,
+                                        0.0, 32 * c, -1), ["ONES"], ["EXP%d" % c])
+
+    def col(k, src, a, b):
+        ts(T.PF[:, k:k + 1], src, a, b, A.mult, A.add, R=["PF"], W=["PF%d" % k])
+
+    def tsc(o, i, k1, k2, o0, o1=None, W=None):
+        R = [nm(i)]
+        sc = []
+        for k in (k1, k2):
+            if isinstance(k, list):
+                R.append("PF%d" % k[0])
+                sc.append(T.PF[:, k[0]:k[0] + 1])
+            else:
+                sc.append(k)
+        ts(o, i, sc[0], sc[1], o0, o1, R=R, W=W)
+
+    col(3, qc, 16.0, 15.0)
+    col(4, qc, 16.0, 1.0)
+    col(5, bc, 1.0, 112.0)
+    col(7, qc, 512.0, 0.0)
+    col(8, pc, -LAM, 63.5 * LAM)
+    ts(T.PF[:, 9:10], bc, 15.0, -16.0, A.is_equal, A.mult, R=["PF"], W=["PF9"])
+    ts(T.MB[:], T.IO[:, 0:16], bc, None, A.is_equal)
+    ts(T.MC[:], T.IO[:, 0:8], qc, None, A.is_equal)
+    tsc(T.XB[:], T.IO[:, 0:144], [4], None, A.is_equal)
+    tsc(T.SB0[:], T.IO[:, 0:240], [5], None, A.is_equal)
+    ts(T.PF[:, 10:11], T.PF[:, 9:10], pc, 1.0, A.add, A.add, R=["PF9"], W=["PF10"])
+    ts(T.PF[:, 11:12], T.PF[:, 7:8], bc, None, A.add, R=["PF7"], W=["PF11"])
+    act(T.WC[:, 0:1], T.PF[:, 8:9], F.Exp, R=["PF8"], W=["WC"])
+    act(T.WC[:, 4:5], T.ONES[:, 0:1], F.Ln, scale=1.0 / BASE, W=["WC4"])
+    ts(T.ID[:], T.IO[:, 0:128], pc, None, A.is_equal)
+    ts(T.IDN[:], T.IO[:, 0:128], pc, -1.0, A.is_equal, A.mult)
+    ts(T.IDB[:], T.IO[:, 0:128], pc, -8192.0, A.is_equal, A.mult)
+    tsc(T.BL[:], T.IO[:, 0:144], [3], 2048.0, A.is_equal, A.mult)
+    ts(T.B8[:], T.MC[:], 2048.0, None, A.mult)
+    ts(T.KROW[:], T.IOF[:], -128.0, 1952.0, A.mult, A.add)
+    ts(T.BROW[:], T.IOF[:], 0.0, -BIG, A.is_equal, A.mult)
+    ms(T.R2K[:], 2048.0)
+    ms(T.DD[:, 0:512:16], -BIG, W=["DD0"])
+    ms(T.DE[:, 0:256:8], 65536.0)
+    for t in range(2):
+        tsc(T.BT[:, 144 * t:144 * t + 144], T.IO[:, 0:144], [3], T.MB[:, t:t + 1], A.is_equal, A.mult, W=["BT%d" % t])
+        ts(T.PF[:, 12 + t:13 + t], bc, float(t), None, A.not_equal, R=["PF"], W=["PF%d" % (12 + t)])
+    tsc(T.P1M[:], T.IO[:, 0:128], [10], None, A.is_equal)
+    ts(T.TR0[:], T.IO[:, 0:128], pc, None, A.is_gt)
+    ts(T.TRI[:], T.ID[:], -1024.0, None, A.mult)
+    for t in range(2):
+        tsc(T.IM[:, 128 * t:128 * t + 128], T.ID[:], [12 + t], None, A.mult, W=["IM%d" % t])
+    ts(T.BON[:], T.IOQ[:], qc, -2048.0, A.is_equal, A.mult)
+    tt(T.TRI[:], T.TRI[:], T.TR0[:], A.add)
+    tt(T.SH[:, 0:128], T.IM[:, 0:128], T.P1M[:], A.subtract, R=["IM0", "P1M"], W=["SH0"])
+    ts(T.ROWS[:], T.OI[:], 0.0, -512.0, A.is_equal, A.mult)
+    ts(T.SH[:, 128:256], T.SH[:, 0:128], -65.0 / 64.0, None, A.mult, R=["SH0"], W=["SH1"])
+    tsc(T.SELF16[:], T.SELF16[:], [11], None, A.add)
+    tsc(T.NR[:], T.NR[:], [7], None, A.add)
+    ts(T.SELF[:], T.SELF16[:], 2048.0, None, A.add)
+    ts(T.SELFK[:], T.SELF16[:], 2048.0, 2048.0, A.add, A.mult)
+    for b in range(16):
+        ts(T.XR[:, 144 * b:144 * b + 144], T.XB[:], T.MB[:, b:b + 1], None, A.mult, W=["XR%d" % b])
+    op("v", lambda: g.vector.reciprocal(T.WC[:, 5:6], T.WC[:, 4:5]), ["WC4"], ["WC5"])
+
+    WK = ["W%d" % q for q in range(8)]
+    NZK = ["NZ%d" % j for j in range(4)]
+    KB = [2, 3, 4, 7]
+
+    def one_round(t):
+        last = t == 1
+        own, new, t16 = T["own%d" % t], T["own%d" % (t + 1)], T["t%d" % t]
+        ko, kt = nm(own[:]), ["t%d0" % t, "t%d1" % t]
+        for q in range(8):
+            mm(P[q % 4][:], T.ES[:, 128 * q:128 * q + 128], own[:], R=["ES%d" % q, ko])
+            if q == 3:
+                for j in (2, 3):
+                    mm(P[4][:, 128 * (j - 2):128 * (j - 1)], own[:, 128 * j:128 * j + 128], T.IDN[:])
+            if q == 7:
+                for i in range(16):
+                    cp(T.OW[:, i::16], own[:, 0:64 * NV], W=["OW%d" % i])
+                cp(T.W[:, 512 * q:512 * q + 512], P[q % 4][:], W=[WK[q]])
+            else:
+                act(T.W[:, 512 * q:512 * q + 512], P[q % 4][:], F.Copy, W=[WK[q]])
+        ts(T.U[:, half[1]], t16[:, half[1]], 2048.0, None, A.add, R=[kt[1]], W=["U1"])
+        OWK = ["OW%d" % i for i in range(16)]
+
+        def vgather(h):
+            tt(T.MX[:, 1024 * h:1024 * h + 1024], T.W[:, 0:4096].indirect(T.U[:, 64 * h:64 * h + 64]),
+               T.OW[:, 1024 * h:1024 * h + 1024], A.max, R=WK + OWK + ["U%d" % (h // 4)],
+               W=["MX%da" % h, "MX%db" % h])
+
+        def sgather(h):
+            k = h - NV
+            act(T.GS[:, 1024 * k:1024 * k + 1024], T.W[:, 0:4096].indirect(T.U[:, 64 * h:64 * h + 64]), F.Copy,
+                R=WK + ["U%d" % (h // 4)], W=["GS%d" % k])
+
+        def sub(h):
+            k = h - NV
+            for x in range(2):
+                c = (2 * h + x) % 4
+                jj = h // 2 - 2
+                mm(P[x][:], T.OT[:, 128 * jj:128 * jj + 128], T.EXP[:, 512 * c:512 * c + 512], True, False,
+                   R=["OT", "EXP%d" % c])
+                mm(P[x][:], T.ID[:], T.GS[:, 1024 * k + 512 * x:1024 * k + 512 * x + 512], False, True,
+                   R=["ID", "GS%d" % k])
+
+        def relu(h):
+            for x in range(2):
+                act(T.MX[:, 1024 * h + 512 * x:1024 * h + 512 * x + 512], P[x][:], F.Relu, W=["MX%d%s" % (h, "ab"[x])])
+
+        def kopen(j):
+            o, c = P[KB[j]][:, 0:128], slice(128 * j, 128 * j + 128)
+            mm(o, t16[:, c], T.ID[:], True, False, R=kt + ["ID"])
+            mm(o, T.HH[:, c], T.IDN[:], False, False)
+            mm(o, T.ONES[0:1, 0:128], T.KROW[0:1, :], False, False)
+            n = min(128, 64 * NV - 128 * j)
+            if n > 0:
+                mm(P[KB[j]][0:n, 0:128], own[:, 128 * j:128 * j + n], T.BON[:], False, False)
+
+        def ksum(j):
+            for i in range(16):
+                mm(P[KB[j]][:, i:128:16], T.MX[:, 2048 * j + i:2048 * j + 2048:16], T.B8[:], False, i == 15,
+                   R=["B8"] + ["MX%d%s" % (h, x) for h in (2 * j, 2 * j + 1) for x in "ab"])
+
+        def kscan(j):
+            for x in range(2):
+                c = slice(512 * x + 128 * j, 512 * x + 128 * j + 128)
+                scan(T.SC[:, c], T.DD[:, c], P[KB[j]][:, 0:128], 0.0, A.add, A.max,
+                     R=["DD%d" % x, "P%d" % KB[j]], W=["SC%d%d" % (x, j)])
+
+        act(T.OT[:], P[4][:, 0:256], F.Copy)
+        sgather(6)
+        vgather(4)
+        sgather(7)
+        ts(T.U[:, half[0]], t16[:, half[0]], 2048.0, None, A.add, R=[kt[0]], W=["U0"])
+        ts(T.HH[:], t16[:], MAGIC, MAGIC, A.add, A.subtract, R=kt)
+        ts(T.TF[:], t16[:], 2048.0 if last else 0.0, None, A.add, R=kt)
+        dma([("y", T.TT[0:16, 512 * q:512 * q + 512], T.TF[16 * q:16 * q + 16, :], ["TF"], ["TTa%d" % q])
+             for q in range(8)])
+        dma([("y", T.TT[16 * q:16 * q + 16, :], T.TT[0:16, :], ["TTa%d" % k for k in range(8)], ["TTb%d" % q])
+             for q in range(1, 8)])
+        TTK = ["TTa%d" % q for q in range(8)] + ["TTb%d" % q for q in range(1, 8)]
+        vgather(0)
+        sub(6)
+        relu(6)
+        kopen(0)
+        for j in range(4):
+            o, c = P[6][:, 128 * j:128 * j + 128], slice(128 * j, 128 * j + 128)
+            mm(o, t16[:, c], T.SH[:, 0:128], True, False, R=kt + ["SH0"])
+            mm(o, T.HH[:, c], T.SH[:, 128:256], False, False, R=["HH", "SH1"])
+            mm(o, T.ONES[0:1, 0:128], T.BROW[0:1, :], False, True)
+        sub(7)
+        sgather(5)
+        vgather(1)
+        kopen(3)
+        kopen(1)
+        kopen(2)
+        ksum(0)
+        relu(7)
+        sub(5)
+        vgather(2)
+        act(T.DD[:, 512:1024], P[6][:], F.Copy, W=["DD1"])
+        relu(5)
+        ksum(3)
+        vgather(3)
+        ksum(2)
+        ksum(1)
+        for j in (0, 3, 2, 1):
+            kscan(j)
+        for b in range(16):
+            mm(P[1][:, 32:64], T.BT[:, 144 * t + 15 - b:144 * t + 143 - b], t16[:, b::16], b == 0, b == 15,
+               R=kt + ["BT%d" % t])
+        for j in (0, 3, 2, 1):
+            act(T.NZ[:, 128 * j:128 * j + 128], P[KB[j]][:, 0:128], F.Sign, bias=-2000.0, W=[NZK[j]])
+
+        S0, S1 = ["SC0%d" % j for j in range(4)], ["SC1%d" % j for j in range(4)]
+        tt(T.TI[:], T.SC[:, 15::16], T.DD[:, 0::16], A.add, R=S0 + S1 + ["DD0", "DD1"])
+        ts(T.NC[:], T.SC[:, 15:512:16], 2048.0, 4096.0, A.is_lt, A.mult, R=S0)
+        ts(T.AI[:], T.TI[:], 127, None, A.bitwise_and)
+        tt(T.X1[:], T.AI[:, 0:32], T.NC[:], A.add)
+        ts(T.U1[:], T.AI[:, 32:64], 64.0, -32.0, A.mult, A.add)
+        tt(T.CM[:], T.U1[:], T.X1[:], A.add)
+        ts(T.SI[:], T.CM[:], 9, None, A.arith_shift_right)
+        ts(T.AU[:], T.CM[:], 4, 31, A.arith_shift_right, A.bitwise_and)
+        ts(T.LO[:], T.CM[:], 15, None, A.bitwise_and)
+        ts(T.OH[:, 0::8], T.SI[:], 0.0, None, A.is_equal, W=["OH0"])
+        cp(T.DH[:, 0:32], T.AU[:])
+        for s in range(1, 8):
+            ts(T.OH[:, s::8], T.SI[:], float(s), None, A.is_equal, W=["OH%d" % s])
+        OHK = ["OH%d" % s for s in range(8)]
+        mm(P[0][:, 0:256], T.ONES[0:1, 0:128], T.ROWS[0:1, :], True, False)
+        mm(P[6][:], T.R2K[0:1, :], T.ONES[0:1, :], True, False)
+        for j in range(4):
+            mm(P[6][:, 128 * j:128 * j + 128], T.NZ[:, 128 * j:128 * j + 128], T.IDB[:], False, False,
+               R=[NZK[j], "IDB"])
+        mm(P[0][:, 0:256], T.TRI[:], T.OH[:], False, False, R=["TRI"] + OHK)
+        for j in (1, 2, 3):
+            mm(P[0][:, 64 * j:256], T.ONES[:, 0:128], T.OH[:, 0:256 - 64 * j], False, j == 3, R=["ONES"] + OHK)
+        for k in range(4):
+            n = 32 << k
+            act(T.DH[:, n:2 * n], T.DH[:, 0:n], F.Identity, bias=-float(1 << k))
+        act(T.ZS[:], T.DH[:], F.Abs, bias=-16.0)
+        act(T.HA[:, 512:1024], T.ZS[:], F.Relu, bias=1.0, scale=-1.0, W=["HA1"])
+        if t == 0:
+            for c in range(8):
+                act(T.SB[:, 240 * c:240 * c + 240], T.SB0[:], F.Identity, scale=T.MC[:, c:c + 1], W=["SB%d" % c])
+        ts(T.S16[:], T.SI[:], 16.0, None, A.mult)
+        ts(T.C16[:], T.CM[:], -2048.0, 2047.0, A.add, A.min)
+        tt(T.PU[:], T.S16[:], T.LO[:], A.add)
+        ts(T.HA[:, 0:512], T.DH[:], 0.0, None, A.is_equal, W=["HA0"])
+        scan(T.EM[:], T.DE[:], P[0][:, 0:256], 0.0, A.add, A.min)
+        ts(T.WT[:], T.EM[:, 7::8], -993.0, T.WC[:, 0:1], A.is_le, A.mult)
+
+        def table(c, h):
+            rho = 31 - (4 * (c % 8) + c // 8)
+            mm(P[2 + h][:, rho::32], T.BB[:, 128 * c:128 * c + 128], T.HA[:, 512 * h + c:512 * h + 512:32],
+               R=["BB%d" % c, "HA%d" % h])
+
+        for c in range(32):
+            ts(T.BB[:, 128 * c:128 * c + 128], T.IO[:, 0:128], T.PU[:, c:c + 1], T.WT[:, c:c + 1], A.is_equal, A.mult,
+               W=["BB%d" % c])
+            table(c, 0)
+            if c > 11:
+                table(c - 12, 1)
+        for c in range(20, 32):
+            table(c, 1)
+        cp(T.TX[:], P[1][:, 32:64])
+        for c in range(8):
+            for q in range(8):
+                mm(P[1][:, c:32:8], T.SB[:, 240 * c + 112 - 16 * q:240 * c + 240 - 16 * q], T.C16[:, q::8],
+                   q == 0, q == 7, R=["SB%d" % c, "C16"])
+        act(T.ZS[:], P[3][:], F.Sign)
+        act(T.Z[:, 512:1024], T.ZS[:], F.Identity, bias=1.0, scale=-1.0, W=["Z1"])
+        ts(T.Z[:, 0:512], P[2][:], 0.0, None, A.is_equal, W=["Z0"])
+        for h in range(2):
+            c = slice(512 * h, 512 * h + 512)
+            scan(T.SC[:, c], T.Z[:, c], P[2 + h][:], 1.0, A.mult, A.add, R=["Z%d" % h, "P%d" % (2 + h)],
+                 W=S1 if h else S0)
+            if h == 1:
+                ts(T.XL[:, 0:32], T.SC[:, 31::32], 1.0, 2.0 ** -20, A.max, A.mult, R=S0 + S1, W=["XL0"])
+                ts(T.XL[:, 32:64], T.SC[:, 31::32], 1.0, 2.0 ** 20, A.min, A.mult, R=S0 + S1, W=["XL1"])
+                act(T.LL[:], T.XL[:], F.Ln, R=["XL0", "XL1"])
+            scan(T.IX[:, c], T.ONES[:], T.Z[:, c], 0.0, A.add, A.mult, R=["ONES", "Z%d" % h], W=["IX%d" % h])
+        IXK = ["IX0", "IX1"]
+        tt(T.Y[:], T.LL[:, 0:32], T.LL[:, 32:64], A.add)
+        ts(T.N128[:], T.IX[:, 31::32], 128.0, -2048.0, A.mult, A.add, R=IXK)
+        ts(T.KI[:], T.Y[:], T.WC[:, 5:6], 63.885, A.mult, A.add, R=["Y", "WC5"])
+        ts(T.HAS2[:], T.IX[:, 31::32], 32.0, -16384.0, A.is_lt, A.mult, R=IXK)
+        tt(T.WN[:], T.KI[:], T.N128[:], A.add)
+        ts(T.AA[:], T.IX[:, 31::32], 32.0, 8192.0, A.is_lt, A.mult, R=IXK)
+        ts(T.WT16[:], T.WN[:], 2048.0, None, A.min)
+        for s in range(8):
+            mm(P[4][:, 32 * s:32 * s + 32], T.ES[:, 128 * s:128 * s + 128], T.WT16[:], R=["ES%d" % s, "WT16"])
+        for b in range(16):
+            mm(P[6][:, b::16], T.XR[:, 144 * b + 1 - t:144 * b + 129 - t], T.HAS2[:], False, b == 15,
+               R=["XR%d" % b, "HAS2"])
+        mm(P[2][:], T.ID[:], own[:])
+        ts(T.CX[:], P[1][:, 0:32], 2048.0, None, A.add)
+        tt(T.AB[:], T.AA[:], T.SELF16[:], A.add)
+        ts(T.CI[:], T.CX[:], 4, None, A.arith_shift_right)
+        tt(T.CL[:], T.WN[:], T.AB[:], A.min)
+        cp(T.IDX[:], T.CI[:])
+        ts(T.CU[:], T.CL[:], 2048.0, None, A.add)
+        cp(T.WN2[:], P[4][:, 0:256])
+        act(T.SA[:], T.W[:, 0:4096].indirect(T.CU[:, 0:32]), F.Copy, R=WK + ["CU"])
+        act(T.ZH[:], P[6][:], F.Relu, bias=-2048.0)
+        tt(T.EQ[:], T.WN2[:, 0:256].indirect(T.IDX[:, 0:32]), T.NR[:], A.is_equal, R=["WN2", "IDX", "NR"])
+        mm(P[7][:], T.IM[:, 128 * t:128 * t + 128], t16[:], True, False, R=kt + ["IM%d" % t])
+        for b in range(16):
+            mm(P[0][:, 0:32], T.BL[:, 15 - b:143 - b], T.EQ[:, b::16], b == 0, b == 15)
+        tt(T.D1[:], T.AA[:], T.TX[:], A.add)
+        tt(T.DX[:], T.CX[:], T.SELF[:], A.subtract)
+        tt(T.NEW[:], T.D1[:], T.WT16[:], A.min)
+        tt(T.NZ[:], T.SA[:], P[2][:], A.max, W=NZK)
+        tt(T.E1[:], P[0][:, 0:32], T.DX[:], A.mult)
+        tt(T.C2[:], T.E1[:], T.SELFK[:], A.add)
+        ts(T.C2U[:], T.C2[:], 1.0 / 2048.0, None, A.mult)
+        for b in range(16):
+            mm(P[7][:, b::16], T.XR[:, 144 * b + 1 - t:144 * b + 129 - t], T.NEW[:], False, False,
+               R=["XR%d" % b, "NEW"])
+        if last:
+            mm(P[7][:], T.R2K[0:1, :], T.ONES[0:1, :], False, False)
+        mm(P[7][:], T.IDN[:], T.ZH[:], False, True)
+        act(T.GT[:], T.TT[:, 0:4096].indirect(T.C2U[:, 0:32]), F.Copy, R=TTK + ["C2U"])
+        tt(new[:], T.W[:, 0:4096].indirect(T.C2U[:, 0:32]), T.NZ[:], A.max, R=WK + NZK + ["C2U"])
+
+        def numbers(out, k):
+            c = half[k]
+            tt(T.EE[:, c], T.GT[:, c], P[6][:, c], A.min, W=["EE%d" % k])
+            tt(out[:, c], T.EE[:, c], P[7][:, c], A.max, R=["EE%d" % k, "P7"], W=[nm(out[:]) + str(k)])
+
+        if last:
+            dma([("y", T.dS[:], new[:], [nm(new[:])], ["dS"])])
+            dma([("s", T.oS[w], new[rows, :], [nm(new[:])], ["oSw"])])
+            for k in range(2):
+                numbers(T.TO, k)
+                dma([("y", T["dT%d" % k][:], T.TO[:, half[k]], ["TO%d" % k], ["dT%d" % k])])
+                dma([("s", T["oT%d" % k][w], T.TO[rows, half[k]], ["TO%d" % k], ["oTw%d" % k])])
+            spread(T.dS, T.oS[w], "aS", ["dS"])
+            for k in range(2):
+                spread(T["dT%d" % k], T["oT%d" % k][w], "aT%d" % k, ["dT%d" % k])
+        else:
+            nxt = cores[(w + 1) % N]
+            rid, pid, _se = topo.addr(nxt)
+            for k in (1, 0):
+                numbers(T.TN, k)
+                need("g", ["TN%d" % k], [])
+                g.remote_dma(T.t1[:, half[k]], T.TN[:, half[k]], T.sem["ah%d" % k], T.sem.ls, pid, rid,
+                             topo.mask(core, nxt))
+                sent[0] += len(topo.engines(core, nxt))
+                total["ah%d" % k] = len(topo.engines(cores[(w - 1) % N], core))
+                wr["t1%d" % k] = ("ah%d" % k, total["ah%d" % k], "r")
+
+    one_round(0)
+    one_round(1)
+    wr["oS"] = ("aS", N - 1, "r")
+    dma([("s", T.ysec[:], T.oS[:], ["oS", "oSw"], ["ysec"])])
+    for k in range(2):
+        wr["oT%d" % k] = ("aT%d" % k, N - 1, "r")
+        dma([("y", T.ytel[:, half[k]], T["oT%d" % k][:], ["oT%d" % k, "oTw%d" % k], ["ytel%d" % k])])
+    total["ls"] = sent[0]
+    total.update(cnt)
+    for s, v in total.items():
+        if seen["g"].get(s, 0) < v:
+            g.wait_ge(T.sem[s], v)

@@ -10,6 +10,8 @@ MAGIC = 1.5 * 2 ** 29
 BASE = 2.2
 LAM = math.log(BASE)
 NV = 5
+GR, LAG = 2, 4
+NG = [0, 2]
 
 SCRATCH = {}
 for _d, _s in (("bfloat16", "dsec lsec dS oS"), ("float16", "dtel ltel")):
@@ -25,7 +27,7 @@ for _d, _s in (
                      "TR0:128 SB:1920" % (1024 * NV, 1024 * (8 - NV))),
         ("float16", "ST16:512 t0:512 t1:512 TN:512 C16:32 WT16:32 NEW:32"),
         ("float32", "TO:512 TT:4096 TF:512 DD:1024 SC:1024 NC:32 U1:32 X1:32 S16:32 PU:32 EM:256 WT:32 XL:64 LL:64 N128:32 "
-                    "AA:32 AB:32 Y:32 WN:32 CL:32 TX:32 D1:32 DX:32 WN2:256 E1:32 C2:32 EE:512 GT:512 "
+                    "AA:32 AB:32 Y:32 CL:32 TX:32 D1:32 DX:32 WN2:256 E1:32 C2:32 EE:512 GT:512 "
                     "PF:16 NR:512 SELF:32 SELF16:32 SELFK:32 MB:16 MC:8 DE:256 WC:8"),
         ("int32", "ST:512 TI:64 AI:64 CM:32 SI:32 LO:32 AU:32 KI:32 CX:32 CI:32 PI:8"),
         ("uint16", "U:512 CU:32 IDX:32 C2U:32")):
@@ -34,7 +36,7 @@ for _d, _s in (
 for _k in range(8):
     SCRATCH["P%d" % _k] = ("psum", [128, 512], "float32")
 
-SEMAPHORES = (["cv", "cs", "cp", "cg", "ls", "asec", "atel", "ah0", "ah1", "aT0", "aT1", "aS"]
+SEMAPHORES = (["cv", "cs", "cp", "cg", "ls", "asec", "atel", "ah0", "ah1", "ah2", "aT0", "aT1", "aS"]
               + ["d%d" % _k for _k in range(22)])
 
 
@@ -128,6 +130,9 @@ def rank_program(g, core, T, topo):
         else:
             op("g", lambda: g.iota(o, pat, base, ch, allow_small_or_imprecise_dtypes=True), [], [nm(o)])
 
+    def gcopy(o, i, n, R, W):
+        op("g", lambda: g.affine_select(o, i, [[0, n]], A.is_equal, 0.0, 0, 0), R, W)
+
     sent = [0]
 
     def spread(src, dst, sem, R):
@@ -146,6 +151,8 @@ def rank_program(g, core, T, topo):
     P = [T["P%d" % k] for k in range(8)]
     rows = slice(16 * w, 16 * w + 16)
     half = [slice(0, 256), slice(256, 512)]
+    part = [slice(192, 448), slice(448, 512), slice(0, 192)]
+    UK = ["U2", "U2", "U2", "U0", "U0", "U0", "U0", "U1"]
 
     dma([("y", T.dsec[:], T.sec[:], [], ["dsec"])])
     dma([("s", T.ST[:], T.tel[:], [], ["ST"])])
@@ -158,15 +165,18 @@ def rank_program(g, core, T, topo):
 
     pc, qc, bc = T.PF[:, 0:1], T.PF[:, 1:2], T.PF[:, 2:3]
     ms(T.ONES[:], 1.0)
-    ms(T.DD[:, 0:512], 0.0, W=["DD0"])
+    ms(T.DD[:, 0:512], 128.0, W=["DD0"])
     ms(T.DE[:], 0.0)
     ts(T.PI[:, 1:2], T.PI[:, 0:1], 4, None, A.arith_shift_right, R=["PI"], W=["PI1"])
     ts(T.PI[:, 2:3], T.PI[:, 0:1], 15, None, A.bitwise_and, R=["PI"], W=["PI2"])
     cp(T.PF[:, 0:3], T.PI[:, 0:3], R=["PI", "PI1", "PI2"])
+    ts(T.PF[:, 8:9], pc, -LAM, 63.5 * LAM, A.mult, A.add, R=["PF"], W=["PF8"])
+    act(T.WC[:, 0:1], T.PF[:, 8:9], F.Exp, R=["PF8"], W=["WC"])
+    act(T.WC[:, 4:5], T.ONES[:, 0:1], F.Ln, scale=1.0 / BASE, W=["WC4"])
     for s in range(8):
         ts(T.ES[:, 128 * s:128 * s + 128], T.IOF[:], float(16 * s), pc, A.add, A.is_equal, W=["ES%d" % s])
     ts(T.ST16[:], T.ST[:], -2048.0, None, A.add)
-    dma([("s", T.dtel[:], T.ST16[:], ["ST16"], ["dtel"])])
+    dma([("y", T.dtel[:], T.ST16[:], ["ST16"], ["dtel"])])
     dma([("y", T.ltel[w], T.ST16[rows, :], ["ST16"], ["ltelw"])])
     iota(T.OI[:], [[0, 4], [1, 8], [-1, 8]], 0, 0)
     iota(T.SELF16[:], [[16, 32]], -2048, 0)
@@ -175,7 +185,7 @@ def rank_program(g, core, T, topo):
     wr["lsec"] = ("asec", N - 1, "r")
     wr["ltel"] = ("atel", N - 1, "r")
     dma([("y", T.own0[:], T.lsec[:], ["lsec", "lsecw"], ["own0"])])
-    dma([("y", T.t0[:], T.ltel[:], ["ltel", "ltelw"], ["t00", "t01"])])
+    dma([("y", T.t0[:], T.ltel[:], ["ltel", "ltelw"], ["t00", "t01", "t02"])])
 
     for c in (0, 1, 2, 3):
         op("g", lambda: g.affine_select(T.EXP[:, 512 * c:512 * c + 512], T.ONES[:], [[1, 32], [0, 16]], A.is_equal,
@@ -199,7 +209,6 @@ def rank_program(g, core, T, topo):
     col(4, qc, 16.0, 1.0)
     col(5, bc, 1.0, 112.0)
     col(7, qc, 512.0, 0.0)
-    col(8, pc, -LAM, 63.5 * LAM)
     ts(T.PF[:, 9:10], bc, 15.0, -16.0, A.is_equal, A.mult, R=["PF"], W=["PF9"])
     ts(T.MB[:], T.IO[:, 0:16], bc, None, A.is_equal)
     ts(T.MC[:], T.IO[:, 0:8], qc, None, A.is_equal)
@@ -207,17 +216,19 @@ def rank_program(g, core, T, topo):
     tsc(T.SB0[:], T.IO[:, 0:240], [5], None, A.is_equal)
     ts(T.PF[:, 10:11], T.PF[:, 9:10], pc, 1.0, A.add, A.add, R=["PF9"], W=["PF10"])
     ts(T.PF[:, 11:12], T.PF[:, 7:8], bc, None, A.add, R=["PF7"], W=["PF11"])
-    act(T.WC[:, 0:1], T.PF[:, 8:9], F.Exp, R=["PF8"], W=["WC"])
-    act(T.WC[:, 4:5], T.ONES[:, 0:1], F.Ln, scale=1.0 / BASE, W=["WC4"])
+    for c in range(8):
+        act(T.SB[:, 240 * c:240 * c + 240], T.SB0[:], F.Identity, scale=T.MC[:, c:c + 1], W=["SB%d" % c])
     ts(T.ID[:], T.IO[:, 0:128], pc, None, A.is_equal)
     ts(T.IDN[:], T.IO[:, 0:128], pc, -1.0, A.is_equal, A.mult)
     ts(T.IDB[:], T.IO[:, 0:128], pc, -8192.0, A.is_equal, A.mult)
     tsc(T.BL[:], T.IO[:, 0:144], [3], 2048.0, A.is_equal, A.mult)
     ts(T.B8[:], T.MC[:], 2048.0, None, A.mult)
-    ts(T.KROW[:], T.IOF[:], -128.0, 1952.0, A.mult, A.add)
-    ts(T.BROW[:], T.IOF[:], 0.0, -BIG, A.is_equal, A.mult)
+    ts(T.PF[:, 6:7], pc, 0.0, 128.0, A.is_equal, A.mult, R=["PF"], W=["PF6"])
+    ts(T.KROW[:], T.IOF[:], 0.0, None, A.is_equal)
+    ts(T.PF[:, 14:15], T.PF[:, 6:7], -(BIG + 160.0) / 128.0, 32.0, A.mult, A.add, R=["PF6"], W=["PF14"])
+    tsc(T.BROW[:], T.KROW[:], [14], [6], A.mult, A.add)
     ms(T.R2K[:], 2048.0)
-    ms(T.DD[:, 0:512:16], -BIG, W=["DD0"])
+    ms(T.DD[:, 0:512:16], 32.0 - BIG, W=["DD0"])
     ms(T.DE[:, 0:256:8], 65536.0)
     for t in range(2):
         tsc(T.BT[:, 144 * t:144 * t + 144], T.IO[:, 0:144], [3], T.MB[:, t:t + 1], A.is_equal, A.mult, W=["BT%d" % t])
@@ -247,7 +258,7 @@ def rank_program(g, core, T, topo):
     def one_round(t):
         last = t == 1
         own, new, t16 = T["own%d" % t], T["own%d" % (t + 1)], T["t%d" % t]
-        ko, kt = nm(own[:]), ["t%d0" % t, "t%d1" % t]
+        ko, kt = nm(own[:]), ["t%d%d" % (t, k) for k in range(3)]
         for q in range(8):
             mm(P[q % 4][:], T.ES[:, 128 * q:128 * q + 128], own[:], R=["ES%d" % q, ko])
             if q == 3:
@@ -255,42 +266,57 @@ def rank_program(g, core, T, topo):
                     mm(P[4][:, 128 * (j - 2):128 * (j - 1)], own[:, 128 * j:128 * j + 128], T.IDN[:])
             if q == 7:
                 for i in range(16):
-                    cp(T.OW[:, i::16], own[:, 0:64 * NV], W=["OW%d" % i])
+                    if i < 16 - NG[t]:
+                        cp(T.OW[:, i::16], own[:, 0:64 * NV], W=["OW%d" % i])
+                    else:
+                        gcopy(T.OW[:, i::16], own[:, 0:64 * NV], 64 * NV, [ko], ["OW%d" % i])
                 cp(T.W[:, 512 * q:512 * q + 512], P[q % 4][:], W=[WK[q]])
-            else:
+                if t == 0:
+                    cp(T.W[:, 512 * 6:512 * 7], P[2][:], W=[WK[6]])
+            elif q < 6 or t == 1:
                 act(T.W[:, 512 * q:512 * q + 512], P[q % 4][:], F.Copy, W=[WK[q]])
-        ts(T.U[:, half[1]], t16[:, half[1]], 2048.0, None, A.add, R=[kt[1]], W=["U1"])
+
+        def offsets(k):
+            ts(T.U[:, part[k]], t16[:, part[k]], 2048.0, None, A.add, R=[kt[k]], W=["U%d" % k])
+
+        offsets(0)
         OWK = ["OW%d" % i for i in range(16)]
 
         def vgather(h):
             tt(T.MX[:, 1024 * h:1024 * h + 1024], T.W[:, 0:4096].indirect(T.U[:, 64 * h:64 * h + 64]),
-               T.OW[:, 1024 * h:1024 * h + 1024], A.max, R=WK + OWK + ["U%d" % (h // 4)],
-               W=["MX%da" % h, "MX%db" % h])
+               T.OW[:, 1024 * h:1024 * h + 1024], A.max, R=WK + OWK + [UK[h]], W=["MX%da" % h, "MX%db" % h])
 
         def sgather(h):
             k = h - NV
             act(T.GS[:, 1024 * k:1024 * k + 1024], T.W[:, 0:4096].indirect(T.U[:, 64 * h:64 * h + 64]), F.Copy,
-                R=WK + ["U%d" % (h // 4)], W=["GS%d" % k])
+                R=WK + [UK[h]], W=["GS%d" % k])
 
-        def sub(h):
+        def bank(h, x):
+            return P[(0, 1, 5)[(2 * (6, 7, 5).index(h) + x) % 3]]
+
+        def sub(h, xs, z=2):
             k = h - NV
-            for x in range(2):
+            for x in xs:
                 c = (2 * h + x) % 4
                 jj = h // 2 - 2
-                mm(P[x][:], T.OT[:, 128 * jj:128 * jj + 128], T.EXP[:, 512 * c:512 * c + 512], True, False,
-                   R=["OT", "EXP%d" % c])
-                mm(P[x][:], T.ID[:], T.GS[:, 1024 * k + 512 * x:1024 * k + 512 * x + 512], False, True,
-                   R=["ID", "GS%d" % k])
+                if z != 1:
+                    mm(bank(h, x)[:], T.OT[:, 128 * jj:128 * jj + 128], T.EXP[:, 512 * c:512 * c + 512], True, False,
+                       R=["OT", "EXP%d" % c])
+                if z != 0:
+                    mm(bank(h, x)[:], T.ID[:], T.GS[:, 1024 * k + 512 * x:1024 * k + 512 * x + 512], False, True,
+                       R=["ID", "GS%d" % k])
 
         def relu(h):
             for x in range(2):
-                act(T.MX[:, 1024 * h + 512 * x:1024 * h + 512 * x + 512], P[x][:], F.Relu, W=["MX%d%s" % (h, "ab"[x])])
+                act(T.MX[:, 1024 * h + 512 * x:1024 * h + 512 * x + 512], bank(h, x)[:], F.Relu,
+                    W=["MX%d%s" % (h, "ab"[x])])
 
-        def kopen(j):
+        def kopen(j, z):
             o, c = P[KB[j]][:, 0:128], slice(128 * j, 128 * j + 128)
+            if z:
+                mm(o, T.HH[:, c], T.IDN[:], False, False)
+                return
             mm(o, t16[:, c], T.ID[:], True, False, R=kt + ["ID"])
-            mm(o, T.HH[:, c], T.IDN[:], False, False)
-            mm(o, T.ONES[0:1, 0:128], T.KROW[0:1, :], False, False)
             n = min(128, 64 * NV - 128 * j)
             if n > 0:
                 mm(P[KB[j]][0:n, 0:128], own[:, 128 * j:128 * j + n], T.BON[:], False, False)
@@ -308,85 +334,95 @@ def rank_program(g, core, T, topo):
 
         act(T.OT[:], P[4][:, 0:256], F.Copy)
         sgather(6)
-        vgather(4)
+        sub(6, (0, 1), 0)
+        sub(7, (0,), 0)
+        for j in (2, 3, 1, 0):
+            kopen(j, 0)
+        vgather(3)
+        offsets(1)
+        offsets(2)
         sgather(7)
-        ts(T.U[:, half[0]], t16[:, half[0]], 2048.0, None, A.add, R=[kt[0]], W=["U0"])
         ts(T.HH[:], t16[:], MAGIC, MAGIC, A.add, A.subtract, R=kt)
-        ts(T.TF[:], t16[:], 2048.0 if last else 0.0, None, A.add, R=kt)
+        gcopy(T.TF[:], t16[:], 512, kt, ["TF"])
         dma([("y", T.TT[0:16, 512 * q:512 * q + 512], T.TF[16 * q:16 * q + 16, :], ["TF"], ["TTa%d" % q])
              for q in range(8)])
         dma([("y", T.TT[16 * q:16 * q + 16, :], T.TT[0:16, :], ["TTa%d" % k for k in range(8)], ["TTb%d" % q])
              for q in range(1, 8)])
         TTK = ["TTa%d" % q for q in range(8)] + ["TTb%d" % q for q in range(1, 8)]
         vgather(0)
-        sub(6)
+        sub(6, (0, 1), 1)
         relu(6)
-        kopen(0)
+        for j in range(4):
+            kopen(j, 1)
         for j in range(4):
             o, c = P[6][:, 128 * j:128 * j + 128], slice(128 * j, 128 * j + 128)
             mm(o, t16[:, c], T.SH[:, 0:128], True, False, R=kt + ["SH0"])
             mm(o, T.HH[:, c], T.SH[:, 128:256], False, False, R=["HH", "SH1"])
-            mm(o, T.ONES[0:1, 0:128], T.BROW[0:1, :], False, True)
-        sub(7)
+            mm(o, T.ONES[0:2, 0:128], T.BROW[0:2, :], False, True)
+        sub(7, (0,), 1)
+        sub(7, (1,))
         sgather(5)
         vgather(1)
-        kopen(3)
-        kopen(1)
-        kopen(2)
+        sub(5, (0,), 0)
         ksum(0)
+        sub(5, (0,), 1)
         relu(7)
-        sub(5)
         vgather(2)
+        sub(5, (1,))
+        ksum(1)
         act(T.DD[:, 512:1024], P[6][:], F.Copy, W=["DD1"])
         relu(5)
         ksum(3)
-        vgather(3)
+        vgather(4)
         ksum(2)
-        ksum(1)
-        for j in (0, 3, 2, 1):
+        for j in (0, 1, 3, 2):
             kscan(j)
         for b in range(16):
             mm(P[1][:, 32:64], T.BT[:, 144 * t + 15 - b:144 * t + 143 - b], t16[:, b::16], b == 0, b == 15,
                R=kt + ["BT%d" % t])
-        for j in (0, 3, 2, 1):
-            act(T.NZ[:, 128 * j:128 * j + 128], P[KB[j]][:, 0:128], F.Sign, bias=-2000.0, W=[NZK[j]])
+
+        def sign(j):
+            act(T.NZ[:, 128 * j:128 * j + 128], P[KB[j]][:, 0:128], F.Sign, bias=-1000.0, W=[NZK[j]])
+
+        sign(0)
+        sign(1)
 
         S0, S1 = ["SC0%d" % j for j in range(4)], ["SC1%d" % j for j in range(4)]
         tt(T.TI[:], T.SC[:, 15::16], T.DD[:, 0::16], A.add, R=S0 + S1 + ["DD0", "DD1"])
-        ts(T.NC[:], T.SC[:, 15:512:16], 2048.0, 4096.0, A.is_lt, A.mult, R=S0)
+        ts(T.NC[:], T.SC[:, 15:512:16], 2000.0, 4096.0, A.is_lt, A.mult, R=S0)
         ts(T.AI[:], T.TI[:], 127, None, A.bitwise_and)
         tt(T.X1[:], T.AI[:, 0:32], T.NC[:], A.add)
         ts(T.U1[:], T.AI[:, 32:64], 64.0, -32.0, A.mult, A.add)
+        ts(T.E1[:], T.AI[:, 32:64], 64.0, -287.5, A.mult, A.add)
         tt(T.CM[:], T.U1[:], T.X1[:], A.add)
-        ts(T.SI[:], T.CM[:], 9, None, A.arith_shift_right)
+        tt(T.C2[:], T.E1[:], T.X1[:], A.add)
         ts(T.AU[:], T.CM[:], 4, 31, A.arith_shift_right, A.bitwise_and)
+        for s in range(8):
+            ts(T.OH[:, s::8], T.C2[:], 8.0 * MAGIC, 8.0 * MAGIC + 512.0 * s, A.add, A.is_equal, W=["OH%d" % s])
+            if s == 1:
+                cp(T.DH[:, 0:32], T.AU[:], W=["DH0"])
+        ts(T.SI[:], T.CM[:], 9, None, A.arith_shift_right)
         ts(T.LO[:], T.CM[:], 15, None, A.bitwise_and)
-        ts(T.OH[:, 0::8], T.SI[:], 0.0, None, A.is_equal, W=["OH0"])
-        cp(T.DH[:, 0:32], T.AU[:])
-        for s in range(1, 8):
-            ts(T.OH[:, s::8], T.SI[:], float(s), None, A.is_equal, W=["OH%d" % s])
         OHK = ["OH%d" % s for s in range(8)]
         mm(P[0][:, 0:256], T.ONES[0:1, 0:128], T.ROWS[0:1, :], True, False)
         mm(P[6][:], T.R2K[0:1, :], T.ONES[0:1, :], True, False)
-        for j in range(4):
-            mm(P[6][:, 128 * j:128 * j + 128], T.NZ[:, 128 * j:128 * j + 128], T.IDB[:], False, False,
-               R=[NZK[j], "IDB"])
         mm(P[0][:, 0:256], T.TRI[:], T.OH[:], False, False, R=["TRI"] + OHK)
         for j in (1, 2, 3):
             mm(P[0][:, 64 * j:256], T.ONES[:, 0:128], T.OH[:, 0:256 - 64 * j], False, j == 3, R=["ONES"] + OHK)
-        for k in range(4):
-            n = 32 << k
-            act(T.DH[:, n:2 * n], T.DH[:, 0:n], F.Identity, bias=-float(1 << k))
-        act(T.ZS[:], T.DH[:], F.Abs, bias=-16.0)
+        DHK = ["DH%d" % k for k in range(7)]
+        for k in (1, 2, 3):
+            act(T.DH[:, 32 * k:32 * k + 32], T.DH[:, 0:32], F.Identity, bias=-float(k), R=["DH0"], W=[DHK[k]])
+        for k in (1, 2, 3):
+            act(T.DH[:, 128 * k:128 * k + 128], T.DH[:, 0:128], F.Identity, bias=-4.0 * k, R=DHK[0:4], W=[DHK[3 + k]])
+        act(T.ZS[:], T.DH[:], F.Abs, bias=-16.0, R=DHK)
+        sign(3)
         act(T.HA[:, 512:1024], T.ZS[:], F.Relu, bias=1.0, scale=-1.0, W=["HA1"])
-        if t == 0:
-            for c in range(8):
-                act(T.SB[:, 240 * c:240 * c + 240], T.SB0[:], F.Identity, scale=T.MC[:, c:c + 1], W=["SB%d" % c])
+        sign(2)
         ts(T.S16[:], T.SI[:], 16.0, None, A.mult)
         ts(T.C16[:], T.CM[:], -2048.0, 2047.0, A.add, A.min)
         tt(T.PU[:], T.S16[:], T.LO[:], A.add)
-        ts(T.HA[:, 0:512], T.DH[:], 0.0, None, A.is_equal, W=["HA0"])
         scan(T.EM[:], T.DE[:], P[0][:, 0:256], 0.0, A.add, A.min)
+        ts(T.HA[:, 0:512], T.DH[:], 0.0, None, A.is_equal, R=DHK, W=["HA0"])
         ts(T.WT[:], T.EM[:, 7::8], -993.0, T.WC[:, 0:1], A.is_le, A.mult)
 
         def table(c, h):
@@ -397,11 +433,18 @@ def rank_program(g, core, T, topo):
         for c in range(32):
             ts(T.BB[:, 128 * c:128 * c + 128], T.IO[:, 0:128], T.PU[:, c:c + 1], T.WT[:, c:c + 1], A.is_equal, A.mult,
                W=["BB%d" % c])
-            table(c, 0)
-            if c > 11:
-                table(c - 12, 1)
-        for c in range(20, 32):
+            if c % GR == GR - 1:
+                need("p", ["BB%d" % c], [])
+                for k in range(c - GR + 1, c + 1):
+                    table(k, 0)
+                if c >= LAG:
+                    for k in range(c - GR + 1 - LAG, c + 1 - LAG):
+                        table(k, 1)
+        for c in range(32 - LAG, 32):
             table(c, 1)
+        for j in range(4):
+            mm(P[6][:, 128 * j:128 * j + 128], T.NZ[:, 128 * j:128 * j + 128], T.IDB[:], False, False,
+               R=[NZK[j], "IDB"])
         cp(T.TX[:], P[1][:, 32:64])
         for c in range(8):
             for q in range(8):
@@ -421,23 +464,24 @@ def rank_program(g, core, T, topo):
             scan(T.IX[:, c], T.ONES[:], T.Z[:, c], 0.0, A.add, A.mult, R=["ONES", "Z%d" % h], W=["IX%d" % h])
         IXK = ["IX0", "IX1"]
         tt(T.Y[:], T.LL[:, 0:32], T.LL[:, 32:64], A.add)
-        ts(T.N128[:], T.IX[:, 31::32], 128.0, -2048.0, A.mult, A.add, R=IXK)
-        ts(T.KI[:], T.Y[:], T.WC[:, 5:6], 63.885, A.mult, A.add, R=["Y", "WC5"])
-        ts(T.HAS2[:], T.IX[:, 31::32], 32.0, -16384.0, A.is_lt, A.mult, R=IXK)
-        tt(T.WN[:], T.KI[:], T.N128[:], A.add)
+        ts(T.N128[:], T.IX[:, 31::32], 32.0, 128.0, A.min, A.mult, R=IXK)
+        ts(T.CX[:], P[1][:, 0:32], 2048.0, None, A.add)
+        ts(T.KI[:], T.Y[:], T.WC[:, 5:6], 63.885 - 2048.0, A.mult, A.add, R=["Y", "WC5"])
         ts(T.AA[:], T.IX[:, 31::32], 32.0, 8192.0, A.is_lt, A.mult, R=IXK)
-        ts(T.WT16[:], T.WN[:], 2048.0, None, A.min)
+        ts(T.CI[:], T.CX[:], 4, None, A.arith_shift_right)
+        tt(T.WT16[:], T.KI[:], T.N128[:], A.add)
+        ts(T.HAS2[:], T.IX[:, 31::32], 32.0, -16384.0, A.is_lt, A.mult, R=IXK)
         for s in range(8):
             mm(P[4][:, 32 * s:32 * s + 32], T.ES[:, 128 * s:128 * s + 128], T.WT16[:], R=["ES%d" % s, "WT16"])
         for b in range(16):
             mm(P[6][:, b::16], T.XR[:, 144 * b + 1 - t:144 * b + 129 - t], T.HAS2[:], False, b == 15,
                R=["XR%d" % b, "HAS2"])
         mm(P[2][:], T.ID[:], own[:])
-        ts(T.CX[:], P[1][:, 0:32], 2048.0, None, A.add)
         tt(T.AB[:], T.AA[:], T.SELF16[:], A.add)
-        ts(T.CI[:], T.CX[:], 4, None, A.arith_shift_right)
-        tt(T.CL[:], T.WN[:], T.AB[:], A.min)
         cp(T.IDX[:], T.CI[:])
+        tt(T.D1[:], T.AA[:], T.TX[:], A.add)
+        tt(T.CL[:], T.WT16[:], T.AB[:], A.min)
+        tt(T.DX[:], T.CX[:], T.SELF[:], A.subtract)
         ts(T.CU[:], T.CL[:], 2048.0, None, A.add)
         cp(T.WN2[:], P[4][:, 0:256])
         act(T.SA[:], T.W[:, 0:4096].indirect(T.CU[:, 0:32]), F.Copy, R=WK + ["CU"])
@@ -446,8 +490,6 @@ def rank_program(g, core, T, topo):
         mm(P[7][:], T.IM[:, 128 * t:128 * t + 128], t16[:], True, False, R=kt + ["IM%d" % t])
         for b in range(16):
             mm(P[0][:, 0:32], T.BL[:, 15 - b:143 - b], T.EQ[:, b::16], b == 0, b == 15)
-        tt(T.D1[:], T.AA[:], T.TX[:], A.add)
-        tt(T.DX[:], T.CX[:], T.SELF[:], A.subtract)
         tt(T.NEW[:], T.D1[:], T.WT16[:], A.min)
         tt(T.NZ[:], T.SA[:], P[2][:], A.max, W=NZK)
         tt(T.E1[:], P[0][:, 0:32], T.DX[:], A.mult)
@@ -459,14 +501,20 @@ def rank_program(g, core, T, topo):
         if last:
             mm(P[7][:], T.R2K[0:1, :], T.ONES[0:1, :], False, False)
         mm(P[7][:], T.IDN[:], T.ZH[:], False, True)
-        act(T.GT[:], T.TT[:, 0:4096].indirect(T.C2U[:, 0:32]), F.Copy, R=TTK + ["C2U"])
+        act(T.GT[:], T.TT[:, 0:4096].indirect(T.C2U[:, 0:32]), F.Identity, bias=2048.0 if last else 0.0,
+            R=TTK + ["C2U"])
         tt(new[:], T.W[:, 0:4096].indirect(T.C2U[:, 0:32]), T.NZ[:], A.max, R=WK + NZK + ["C2U"])
 
-        def numbers(out, k):
-            c = half[k]
+        def low(k):
+            c = half[k] if last else part[k]
             tt(T.EE[:, c], T.GT[:, c], P[6][:, c], A.min, W=["EE%d" % k])
+
+        def numbers(out, k):
+            c = half[k] if last else part[k]
             tt(out[:, c], T.EE[:, c], P[7][:, c], A.max, R=["EE%d" % k, "P7"], W=[nm(out[:]) + str(k)])
 
+        low(0)
+        low(1)
         if last:
             dma([("y", T.dS[:], new[:], [nm(new[:])], ["dS"])])
             dma([("s", T.oS[w], new[rows, :], [nm(new[:])], ["oSw"])])
@@ -480,10 +528,12 @@ def rank_program(g, core, T, topo):
         else:
             nxt = cores[(w + 1) % N]
             rid, pid, _se = topo.addr(nxt)
-            for k in (1, 0):
+            for k in range(3):
                 numbers(T.TN, k)
+                if k == 0:
+                    low(2)
                 need("g", ["TN%d" % k], [])
-                g.remote_dma(T.t1[:, half[k]], T.TN[:, half[k]], T.sem["ah%d" % k], T.sem.ls, pid, rid,
+                g.remote_dma(T.t1[:, part[k]], T.TN[:, part[k]], T.sem["ah%d" % k], T.sem.ls, pid, rid,
                              topo.mask(core, nxt))
                 sent[0] += len(topo.engines(core, nxt))
                 total["ah%d" % k] = len(topo.engines(cores[(w - 1) % N], core))

import math
from concourse.bass import DstId, RemoteDMATransfer
from concourse.mybir import AluOpType, ActivationFunctionType

A = AluOpType
F = ActivationFunctionType
N = 8
BIG = float(2 ** 23)
MAGIC = 1.5 * 2 ** 29
BASE = 2.2
LAM = math.log(BASE)
NV = 5
GR, LAG = 2, 4
NG = [0, 2]

SCRATCH = {}
for _d, _s in (("bfloat16", "dsec lsec dS oS"), ("float16", "dtel ltel")):
    for _k in _s.split():
        SCRATCH[_k] = ("dram", [8, 128, 64], _d)
for _k in ("dT0", "dT1", "oT0", "oT1"):
    SCRATCH[_k] = ("dram", [8, 128, 32], "float32")
for _d, _s in (
        ("bfloat16", "own0:512 own1:512 own2:512 W:4096 OW:%d MX:8192 GS:%d OT:256 HH:512 OH:256 DH:512 HA:1024 BB:4096 "
                     "Z:1024 ZS:512 IX:1024 HAS2:32 EQ:512 NZ:512 SA:512 ZH:512 "
                     "IO:256 IOF:128 IOQ:128 EXP:2048 OI:256 ROWS:256 BROW:128 KROW:128 ONES:512 R2K:128 ID:128 IDN:128 "
                     "IDB:128 ES:1024 BL:144 BON:128 B8:8 XB:144 SB0:240 XR:2304 BT:288 IM:256 P1M:128 SH:256 TRI:128 "
                     "TR0:128 SB:1920" % (1024 * NV, 1024 * (8 - NV))),
        ("float16", "ST16:512 t0:512 t1:512 TN:512 C16:32 WT16:32 NEW:32"),
        ("float32", "TO:512 TT:4096 TF:512 DD:1024 SC:1024 NC:32 U1:32 X1:32 S16:32 PU:32 EM:256 WT:32 XL:64 LL:64 N128:32 "
                    "AA:32 AB:32 Y:32 CL:32 TX:32 D1:32 DX:32 WN2:256 E1:32 C2:32 EE:512 GT:512 "
                    "PF:16 NR:512 SELF:32 SELF16:32 SELFK:32 MB:16 MC:8 DE:256 WC:8"),
        ("int32", "ST:512 TI:64 AI:64 CM:32 SI:32 LO:32 AU:32 KI:32 CX:32 CI:32 PI:8"),
        ("uint16", "U:512 CU:32 IDX:32 C2U:32")):
    for _k in _s.split():
        SCRATCH[_k.split(":")[0]] = ("sbuf", [128, int(_k.split(":")[1])], _d)
for _k in range(8):
    SCRATCH["P%d" % _k] = ("psum", [128, 512], "float32")

SEMAPHORES = (["cv", "cs", "cp", "cg", "ls", "asec", "atel", "ah0", "ah1", "ah2", "aT0", "aT1", "aS"]
              + ["d%d" % _k for _k in range(22)])


def rank_program(g, core, T, topo):
    w = T.rank_of(core)
    if w is None:
        return
    cores = list(T.cores)
    Q = {"v": g.vector, "s": g.scalar, "p": g.tensor, "g": g, "y": g.sync}
    cnt = {"cv": 0, "cs": 0, "cp": 0, "cg": 0}
    seen = {e: {} for e in Q}
    wr, rd, total, nd = {}, {}, {}, [0]
    names = {T[k].name: k for k in SCRATCH}

    def need(e, R, W):
        toks = []
        for k in R:
            if k in wr:
                toks.append(wr[k])
            if k[0] == "P" and k[1:].isdigit():
                toks += [t for t in rd.get(k, []) if t[2] != e]
        for k in W:
            toks += [t for t in rd.get(k, []) + ([wr[k]] if k in wr else []) if t[2] != e or e != "p"]
        top = {}
        for s, v, _e in toks:
            top[s] = max(top.get(s, 0), v)
        for s, v in top.items():
            if seen[e].get(s, 0) < v:
                Q[e].wait_ge(T.sem[s], v)
                seen[e][s] = v

    def mark(tok, R, W):
        for k in R:
            rd.setdefault(k, []).append(tok)
        for k in W:
            wr[k] = tok
            rd[k] = []

    def op(e, fn, R, W):
        need(e, R, W)
        s = "c" + e
        cnt[s] += 1
        fn().then_inc(T.sem[s], 1)
        mark((s, cnt[s], e), R, W)

    def dma(items):
        s = "d%d" % nd[0]
        nd[0] += 1
        for e, o, i, R, W in items:
            need(e, R, W)
            Q[e].dma_start(o, i).then_inc(T.sem[s], 16)
        total[s] = 16 * len(items)
        for e, o, i, R, W in items:
            mark((s, total[s], "d"), R, W)

    def nm(ap):
        return names[ap.name]

    def cols(*xs):
        return [nm(s) for s in xs if s is not None and not isinstance(s, (int, float))]

    def ts(o, i, s1, s2, o0, o1=None, R=None, W=None):
        r = (list(R) if R else [nm(i)]) + cols(s1, s2)
        if o1 is None:
            op("v", lambda: g.vector.tensor_scalar(o, i, s1, None, o0), r, W or [nm(o)])
        else:
            op("v", lambda: g.vector.tensor_scalar(o, i, s1, s2, o0, o1), r, W or [nm(o)])

    def tt(o, a, b, o0, R=None, W=None):
        op("v", lambda: g.vector.tensor_tensor(o, a, b, o0), R or [nm(a), nm(b)], W or [nm(o)])

    def cp(o, i, R=None, W=None):
        op("v", lambda: g.vector.tensor_copy(o, i), R or [nm(i)], W or [nm(o)])

    def ms(o, c, W=None):
        op("v", lambda: g.vector.memset(o, c), [], W or [nm(o)])

    def scan(o, d0, d1, init, o0, o1, R=None, W=None):
        op("v", lambda: g.vector.tensor_tensor_scan(o, d0, d1, init, o0, o1), R or [nm(d0), nm(d1)], W or [nm(o)])

    def act(o, i, f, bias=0.0, scale=1.0, R=None, W=None):
        r = (list(R) if R else [nm(i)]) + cols(bias, scale)
        op("s", lambda: g.scalar.activation(o, i, f, bias=bias, scale=scale), r, W or [nm(o)])

    def mm(o, l, r, a=True, z=True, R=None):
        op("p", lambda: g.tensor.matmul(o, l, r, a, z), R or [nm(l), nm(r)], [nm(o)])

    def iota(o, pat, base, ch):
        if nm(o) == "PI":
            op("g", lambda: g.iota(o, pat, base, ch), [], [nm(o)])
        else:
            op("g", lambda: g.iota(o, pat, base, ch, allow_small_or_imprecise_dtypes=True), [], [nm(o)])

    def gcopy(o, i, n, R, W):
        op("g", lambda: g.affine_select(o, i, [[0, n]], A.is_equal, 0.0, 0, 0), R, W)

    sent = [0]

    def spread(src, dst, sem, R):
        need("g", R, [])
        tr = []
        for k in range(1, N):
            r = (w + k) % N
            rid, pid, _se = topo.addr(cores[r])
            tr.append(RemoteDMATransfer(dst_ids=[DstId(rid=rid, pnc=pid)],
                                        dma_engine_mask=1 << topo.engines(core, cores[r])[k - 1],
                                        remote_sem=T.sem[sem], src=src[r], dst=dst))
        g.remote_dma_fused(tr, local_sem=T.sem.ls)
        sent[0] += N - 1
        total[sem] = N - 1

    P = [T["P%d" % k] for k in range(8)]
    rows = slice(16 * w, 16 * w + 16)
    half = [slice(0, 256), slice(256, 512)]
    part = [slice(192, 448), slice(448, 512), slice(0, 192)]
    UK = ["U2", "U2", "U2", "U0", "U0", "U0", "U0", "U1"]

    dma([("y", T.dsec[:], T.sec[:], [], ["dsec"])])
    dma([("s", T.ST[:], T.tel[:], [], ["ST"])])
    dma([("y", T.lsec[w], T.sec[rows, :], [], ["lsecw"])])
    iota(T.IO[:], [[1, 256]], 0, 0)
    iota(T.PI[:, 0:1], [[1, 1]], 0, 1)
    iota(T.IOF[:], [[0, 8], [1, 16]], 0, 0)
    iota(T.IOQ[:], [[1, 8], [0, 16]], 0, 0)
    spread(T.dsec, T.lsec[w], "asec", ["dsec"])

    pc, qc, bc = T.PF[:, 0:1], T.PF[:, 1:2], T.PF[:, 2:3]
    ms(T.ONES[:], 1.0)
    ms(T.DD[:, 0:512], 128.0, W=["DD0"])
    ms(T.DE[:], 0.0)
    ts(T.PI[:, 1:2], T.PI[:, 0:1], 4, None, A.arith_shift_right, R=["PI"], W=["PI1"])
    ts(T.PI[:, 2:3], T.PI[:, 0:1], 15, None, A.bitwise_and, R=["PI"], W=["PI2"])
    cp(T.PF[:, 0:3], T.PI[:, 0:3], R=["PI", "PI1", "PI2"])
    ts(T.PF[:, 8:9], pc, -LAM, 63.5 * LAM, A.mult, A.add, R=["PF"], W=["PF8"])
    act(T.WC[:, 0:1], T.PF[:, 8:9], F.Exp, R=["PF8"], W=["WC"])
    act(T.WC[:, 4:5], T.ONES[:, 0:1], F.Ln, scale=1.0 / BASE, W=["WC4"])
    for s in range(8):
        ts(T.ES[:, 128 * s:128 * s + 128], T.IOF[:], float(16 * s), pc, A.add, A.is_equal, W=["ES%d" % s])
    ts(T.ST16[:], T.ST[:], -2048.0, None, A.add)
    dma([("y", T.dtel[:], T.ST16[:], ["ST16"], ["dtel"])])
    dma([("y", T.ltel[w], T.ST16[rows, :], ["ST16"], ["ltelw"])])
    iota(T.OI[:], [[0, 4], [1, 8], [-1, 8]], 0, 0)
    iota(T.SELF16[:], [[16, 32]], -2048, 0)
    iota(T.NR[:], [[1, 512]], -2048, 0)
    spread(T.dtel, T.ltel[w], "atel", ["dtel"])
    wr["lsec"] = ("asec", N - 1, "r")
    wr["ltel"] = ("atel", N - 1, "r")
    dma([("y", T.own0[:], T.lsec[:], ["lsec", "lsecw"], ["own0"])])
    dma([("y", T.t0[:], T.ltel[:], ["ltel", "ltelw"], ["t00", "t01", "t02"])])

    for c in (0, 1, 2, 3):
        op("g", lambda: g.affine_select(T.EXP[:, 512 * c:512 * c + 512], T.ONES[:], [[1, 32], [0, 16]], A.is_equal,
                                        0.0, 32 * c, -1), ["ONES"], ["EXP%d" % c])

    def col(k, src, a, b):
        ts(T.PF[:, k:k + 1], src, a, b, A.mult, A.add, R=["PF"], W=["PF%d" % k])

    def tsc(o, i, k1, k2, o0, o1=None, W=None):
        R = [nm(i)]
        sc = []
        for k in (k1, k2):
            if isinstance(k, list):
                R.append("PF%d" % k[0])
                sc.append(T.PF[:, k[0]:k[0] + 1])
            else:
                sc.append(k)
        ts(o, i, sc[0], sc[1], o0, o1, R=R, W=W)

    col(3, qc, 16.0, 15.0)
    col(4, qc, 16.0, 1.0)
    col(5, bc, 1.0, 112.0)
    col(7, qc, 512.0, 0.0)
    ts(T.PF[:, 9:10], bc, 15.0, -16.0, A.is_equal, A.mult, R=["PF"], W=["PF9"])
    ts(T.MB[:], T.IO[:, 0:16], bc, None, A.is_equal)
    ts(T.MC[:], T.IO[:, 0:8], qc, None, A.is_equal)
    tsc(T.XB[:], T.IO[:, 0:144], [4], None, A.is_equal)
    tsc(T.SB0[:], T.IO[:, 0:240], [5], None, A.is_equal)
    ts(T.PF[:, 10:11], T.PF[:, 9:10], pc, 1.0, A.add, A.add, R=["PF9"], W=["PF10"])
    ts(T.PF[:, 11:12], T.PF[:, 7:8], bc, None, A.add, R=["PF7"], W=["PF11"])
    for c in range(8):
        act(T.SB[:, 240 * c:240 * c + 240], T.SB0[:], F.Identity, scale=T.MC[:, c:c + 1], W=["SB%d" % c])
    ts(T.ID[:], T.IO[:, 0:128], pc, None, A.is_equal)
    ts(T.IDN[:], T.IO[:, 0:128], pc, -1.0, A.is_equal, A.mult)
    ts(T.IDB[:], T.IO[:, 0:128], pc, -8192.0, A.is_equal, A.mult)
    tsc(T.BL[:], T.IO[:, 0:144], [3], 2048.0, A.is_equal, A.mult)
    ts(T.B8[:], T.MC[:], 2048.0, None, A.mult)
    ts(T.PF[:, 6:7], pc, 0.0, 128.0, A.is_equal, A.mult, R=["PF"], W=["PF6"])
    ts(T.KROW[:], T.IOF[:], 0.0, None, A.is_equal)
    ts(T.PF[:, 14:15], T.PF[:, 6:7], -(BIG + 160.0) / 128.0, 32.0, A.mult, A.add, R=["PF6"], W=["PF14"])
    tsc(T.BROW[:], T.KROW[:], [14], [6], A.mult, A.add)
    ms(T.R2K[:], 2048.0)
    ms(T.DD[:, 0:512:16], 32.0 - BIG, W=["DD0"])
    ms(T.DE[:, 0:256:8], 65536.0)
    for t in range(2):
        tsc(T.BT[:, 144 * t:144 * t + 144], T.IO[:, 0:144], [3], T.MB[:, t:t + 1], A.is_equal, A.mult, W=["BT%d" % t])
        ts(T.PF[:, 12 + t:13 + t], bc, float(t), None, A.not_equal, R=["PF"], W=["PF%d" % (12 + t)])
    tsc(T.P1M[:], T.IO[:, 0:128], [10], None, A.is_equal)
    ts(T.TR0[:], T.IO[:, 0:128], pc, None, A.is_gt)
    ts(T.TRI[:], T.ID[:], -1024.0, None, A.mult)
    for t in range(2):
        tsc(T.IM[:, 128 * t:128 * t + 128], T.ID[:], [12 + t], None, A.mult, W=["IM%d" % t])
    ts(T.BON[:], T.IOQ[:], qc, -2048.0, A.is_equal, A.mult)
    tt(T.TRI[:], T.TRI[:], T.TR0[:], A.add)
    tt(T.SH[:, 0:128], T.IM[:, 0:128], T.P1M[:], A.subtract, R=["IM0", "P1M"], W=["SH0"])
    ts(T.ROWS[:], T.OI[:], 0.0, -512.0, A.is_equal, A.mult)
    ts(T.SH[:, 128:256], T.SH[:, 0:128], -65.0 / 64.0, None, A.mult, R=["SH0"], W=["SH1"])
    tsc(T.SELF16[:], T.SELF16[:], [11], None, A.add)
    tsc(T.NR[:], T.NR[:], [7], None, A.add)
    ts(T.SELF[:], T.SELF16[:], 2048.0, None, A.add)
    ts(T.SELFK[:], T.SELF16[:], 2048.0, 2048.0, A.add, A.mult)
    for b in range(16):
        ts(T.XR[:, 144 * b:144 * b + 144], T.XB[:], T.MB[:, b:b + 1], None, A.mult, W=["XR%d" % b])
    op("v", lambda: g.vector.reciprocal(T.WC[:, 5:6], T.WC[:, 4:5]), ["WC4"], ["WC5"])

    WK = ["W%d" % q for q in range(8)]
    NZK = ["NZ%d" % j for j in range(4)]
    KB = [2, 3, 4, 7]

    def one_round(t):
        last = t == 1
        own, new, t16 = T["own%d" % t], T["own%d" % (t + 1)], T["t%d" % t]
        ko, kt = nm(own[:]), ["t%d%d" % (t, k) for k in range(3)]
        for q in range(8):
            mm(P[q % 4][:], T.ES[:, 128 * q:128 * q + 128], own[:], R=["ES%d" % q, ko])
            if q == 3:
                for j in (2, 3):
                    mm(P[4][:, 128 * (j - 2):128 * (j - 1)], own[:, 128 * j:128 * j + 128], T.IDN[:])
            if q == 7:
                for i in range(16):
                    if i < 16 - NG[t]:
                        cp(T.OW[:, i::16], own[:, 0:64 * NV], W=["OW%d" % i])
                    else:
                        gcopy(T.OW[:, i::16], own[:, 0:64 * NV], 64 * NV, [ko], ["OW%d" % i])
                cp(T.W[:, 512 * q:512 * q + 512], P[q % 4][:], W=[WK[q]])
                if t == 0:
                    cp(T.W[:, 512 * 6:512 * 7], P[2][:], W=[WK[6]])
            elif q < 6 or t == 1:
                act(T.W[:, 512 * q:512 * q + 512], P[q % 4][:], F.Copy, W=[WK[q]])

        def offsets(k):
            ts(T.U[:, part[k]], t16[:, part[k]], 2048.0, None, A.add, R=[kt[k]], W=["U%d" % k])

        offsets(0)
        OWK = ["OW%d" % i for i in range(16)]

        def vgather(h):
            tt(T.MX[:, 1024 * h:1024 * h + 1024], T.W[:, 0:4096].indirect(T.U[:, 64 * h:64 * h + 64]),
               T.OW[:, 1024 * h:1024 * h + 1024], A.max, R=WK + OWK + [UK[h]], W=["MX%da" % h, "MX%db" % h])

        def sgather(h):
            k = h - NV
            act(T.GS[:, 1024 * k:1024 * k + 1024], T.W[:, 0:4096].indirect(T.U[:, 64 * h:64 * h + 64]), F.Copy,
                R=WK + [UK[h]], W=["GS%d" % k])

        def bank(h, x):
            return P[(0, 1, 5)[(2 * (6, 7, 5).index(h) + x) % 3]]

        def sub(h, xs, z=2):
            k = h - NV
            for x in xs:
                c = (2 * h + x) % 4
                jj = h // 2 - 2
                if z != 1:
                    mm(bank(h, x)[:], T.OT[:, 128 * jj:128 * jj + 128], T.EXP[:, 512 * c:512 * c + 512], True, False,
                       R=["OT", "EXP%d" % c])
                if z != 0:
                    mm(bank(h, x)[:], T.ID[:], T.GS[:, 1024 * k + 512 * x:1024 * k + 512 * x + 512], False, True,
                       R=["ID", "GS%d" % k])

        def relu(h):
            for x in range(2):
                act(T.MX[:, 1024 * h + 512 * x:1024 * h + 512 * x + 512], bank(h, x)[:], F.Relu,
                    W=["MX%d%s" % (h, "ab"[x])])

        def kopen(j, z):
            o, c = P[KB[j]][:, 0:128], slice(128 * j, 128 * j + 128)
            if z:
                mm(o, T.HH[:, c], T.IDN[:], False, False)
                return
            mm(o, t16[:, c], T.ID[:], True, False, R=kt + ["ID"])
            n = min(128, 64 * NV - 128 * j)
            if n > 0:
                mm(P[KB[j]][0:n, 0:128], own[:, 128 * j:128 * j + n], T.BON[:], False, False)

        def ksum(j):
            for i in range(16):
                mm(P[KB[j]][:, i:128:16], T.MX[:, 2048 * j + i:2048 * j + 2048:16], T.B8[:], False, i == 15,
                   R=["B8"] + ["MX%d%s" % (h, x) for h in (2 * j, 2 * j + 1) for x in "ab"])

        def kscan(j):
            for x in range(2):
                c = slice(512 * x + 128 * j, 512 * x + 128 * j + 128)
                scan(T.SC[:, c], T.DD[:, c], P[KB[j]][:, 0:128], 0.0, A.add, A.max,
                     R=["DD%d" % x, "P%d" % KB[j]], W=["SC%d%d" % (x, j)])

        act(T.OT[:], P[4][:, 0:256], F.Copy)
        sgather(6)
        sub(6, (0, 1), 0)
        sub(7, (0,), 0)
        for j in (2, 3, 1, 0):
            kopen(j, 0)
        vgather(3)
        offsets(1)
        offsets(2)
        sgather(7)
        ts(T.HH[:], t16[:], MAGIC, MAGIC, A.add, A.subtract, R=kt)
        gcopy(T.TF[:], t16[:], 512, kt, ["TF"])
        dma([("y", T.TT[0:16, 512 * q:512 * q + 512], T.TF[16 * q:16 * q + 16, :], ["TF"], ["TTa%d" % q])
             for q in range(8)])
        dma([("y", T.TT[16 * q:16 * q + 16, :], T.TT[0:16, :], ["TTa%d" % k for k in range(8)], ["TTb%d" % q])
             for q in range(1, 8)])
        TTK = ["TTa%d" % q for q in range(8)] + ["TTb%d" % q for q in range(1, 8)]
        vgather(0)
        sub(6, (0, 1), 1)
        relu(6)
        for j in range(4):
            kopen(j, 1)
        for j in range(4):
            o, c = P[6][:, 128 * j:128 * j + 128], slice(128 * j, 128 * j + 128)
            mm(o, t16[:, c], T.SH[:, 0:128], True, False, R=kt + ["SH0"])
            mm(o, T.HH[:, c], T.SH[:, 128:256], False, False, R=["HH", "SH1"])
            mm(o, T.ONES[0:2, 0:128], T.BROW[0:2, :], False, True)
        sub(7, (0,), 1)
        sub(7, (1,))
        sgather(5)
        vgather(1)
        sub(5, (0,), 0)
        ksum(0)
        sub(5, (0,), 1)
        relu(7)
        vgather(2)
        sub(5, (1,))
        ksum(1)
        act(T.DD[:, 512:1024], P[6][:], F.Copy, W=["DD1"])
        relu(5)
        ksum(3)
        vgather(4)
        ksum(2)
        for j in (0, 1, 3, 2):
            kscan(j)
        for b in range(16):
            mm(P[1][:, 32:64], T.BT[:, 144 * t + 15 - b:144 * t + 143 - b], t16[:, b::16], b == 0, b == 15,
               R=kt + ["BT%d" % t])

        def sign(j):
            act(T.NZ[:, 128 * j:128 * j + 128], P[KB[j]][:, 0:128], F.Sign, bias=-1000.0, W=[NZK[j]])

        sign(0)
        sign(1)

        S0, S1 = ["SC0%d" % j for j in range(4)], ["SC1%d" % j for j in range(4)]
        tt(T.TI[:], T.SC[:, 15::16], T.DD[:, 0::16], A.add, R=S0 + S1 + ["DD0", "DD1"])
        ts(T.NC[:], T.SC[:, 15:512:16], 2000.0, 4096.0, A.is_lt, A.mult, R=S0)
        ts(T.AI[:], T.TI[:], 127, None, A.bitwise_and)
        tt(T.X1[:], T.AI[:, 0:32], T.NC[:], A.add)
        ts(T.U1[:], T.AI[:, 32:64], 64.0, -32.0, A.mult, A.add)
        ts(T.E1[:], T.AI[:, 32:64], 64.0, -287.5, A.mult, A.add)
        tt(T.CM[:], T.U1[:], T.X1[:], A.add)
        tt(T.C2[:], T.E1[:], T.X1[:], A.add)
        ts(T.AU[:], T.CM[:], 4, 31, A.arith_shift_right, A.bitwise_and)
        for s in range(8):
            ts(T.OH[:, s::8], T.C2[:], 8.0 * MAGIC, 8.0 * MAGIC + 512.0 * s, A.add, A.is_equal, W=["OH%d" % s])
            if s == 1:
                cp(T.DH[:, 0:32], T.AU[:], W=["DH0"])
        ts(T.SI[:], T.CM[:], 9, None, A.arith_shift_right)
        ts(T.LO[:], T.CM[:], 15, None, A.bitwise_and)
        OHK = ["OH%d" % s for s in range(8)]
        mm(P[0][:, 0:256], T.ONES[0:1, 0:128], T.ROWS[0:1, :], True, False)
        mm(P[6][:], T.R2K[0:1, :], T.ONES[0:1, :], True, False)
        mm(P[0][:, 0:256], T.TRI[:], T.OH[:], False, False, R=["TRI"] + OHK)
        for j in (1, 2, 3):
            mm(P[0][:, 64 * j:256], T.ONES[:, 0:128], T.OH[:, 0:256 - 64 * j], False, j == 3, R=["ONES"] + OHK)
        DHK = ["DH%d" % k for k in range(7)]
        for k in (1, 2, 3):
            act(T.DH[:, 32 * k:32 * k + 32], T.DH[:, 0:32], F.Identity, bias=-float(k), R=["DH0"], W=[DHK[k]])
        for k in (1, 2, 3):
            act(T.DH[:, 128 * k:128 * k + 128], T.DH[:, 0:128], F.Identity, bias=-4.0 * k, R=DHK[0:4], W=[DHK[3 + k]])
        act(T.ZS[:], T.DH[:], F.Abs, bias=-16.0, R=DHK)
        sign(3)
        act(T.HA[:, 512:1024], T.ZS[:], F.Relu, bias=1.0, scale=-1.0, W=["HA1"])
        sign(2)
        ts(T.S16[:], T.SI[:], 16.0, None, A.mult)
        ts(T.C16[:], T.CM[:], -2048.0, 2047.0, A.add, A.min)
        tt(T.PU[:], T.S16[:], T.LO[:], A.add)
        scan(T.EM[:], T.DE[:], P[0][:, 0:256], 0.0, A.add, A.min)
        ts(T.HA[:, 0:512], T.DH[:], 0.0, None, A.is_equal, R=DHK, W=["HA0"])
        ts(T.WT[:], T.EM[:, 7::8], -993.0, T.WC[:, 0:1], A.is_le, A.mult)

        def table(c, h):
            rho = 31 - (4 * (c % 8) + c // 8)
            mm(P[2 + h][:, rho::32], T.BB[:, 128 * c:128 * c + 128], T.HA[:, 512 * h + c:512 * h + 512:32],
               R=["BB%d" % c, "HA%d" % h])

        for c in range(32):
            ts(T.BB[:, 128 * c:128 * c + 128], T.IO[:, 0:128], T.PU[:, c:c + 1], T.WT[:, c:c + 1], A.is_equal, A.mult,
               W=["BB%d" % c])
            if c % GR == GR - 1:
                need("p", ["BB%d" % c], [])
                for k in range(c - GR + 1, c + 1):
                    table(k, 0)
                if c >= LAG:
                    for k in range(c - GR + 1 - LAG, c + 1 - LAG):
                        table(k, 1)
        for c in range(32 - LAG, 32):
            table(c, 1)
        for j in range(4):
            mm(P[6][:, 128 * j:128 * j + 128], T.NZ[:, 128 * j:128 * j + 128], T.IDB[:], False, False,
               R=[NZK[j], "IDB"])
        cp(T.TX[:], P[1][:, 32:64])
        for c in range(8):
            for q in range(8):
                mm(P[1][:, c:32:8], T.SB[:, 240 * c + 112 - 16 * q:240 * c + 240 - 16 * q], T.C16[:, q::8],
                   q == 0, q == 7, R=["SB%d" % c, "C16"])
        act(T.ZS[:], P[3][:], F.Sign)
        act(T.Z[:, 512:1024], T.ZS[:], F.Identity, bias=1.0, scale=-1.0, W=["Z1"])
        ts(T.Z[:, 0:512], P[2][:], 0.0, None, A.is_equal, W=["Z0"])
        for h in range(2):
            c = slice(512 * h, 512 * h + 512)
            scan(T.SC[:, c], T.Z[:, c], P[2 + h][:], 1.0, A.mult, A.add, R=["Z%d" % h, "P%d" % (2 + h)],
                 W=S1 if h else S0)
            if h == 1:
                ts(T.XL[:, 0:32], T.SC[:, 31::32], 1.0, 2.0 ** -20, A.max, A.mult, R=S0 + S1, W=["XL0"])
                ts(T.XL[:, 32:64], T.SC[:, 31::32], 1.0, 2.0 ** 20, A.min, A.mult, R=S0 + S1, W=["XL1"])
                act(T.LL[:], T.XL[:], F.Ln, R=["XL0", "XL1"])
            scan(T.IX[:, c], T.ONES[:], T.Z[:, c], 0.0, A.add, A.mult, R=["ONES", "Z%d" % h], W=["IX%d" % h])
        IXK = ["IX0", "IX1"]
        tt(T.Y[:], T.LL[:, 0:32], T.LL[:, 32:64], A.add)
        ts(T.N128[:], T.IX[:, 31::32], 32.0, 128.0, A.min, A.mult, R=IXK)
        ts(T.CX[:], P[1][:, 0:32], 2048.0, None, A.add)
        ts(T.KI[:], T.Y[:], T.WC[:, 5:6], 63.885 - 2048.0, A.mult, A.add, R=["Y", "WC5"])
        ts(T.AA[:], T.IX[:, 31::32], 32.0, 8192.0, A.is_lt, A.mult, R=IXK)
        ts(T.CI[:], T.CX[:], 4, None, A.arith_shift_right)
        tt(T.WT16[:], T.KI[:], T.N128[:], A.add)
        ts(T.HAS2[:], T.IX[:, 31::32], 32.0, -16384.0, A.is_lt, A.mult, R=IXK)
        for s in range(8):
            mm(P[4][:, 32 * s:32 * s + 32], T.ES[:, 128 * s:128 * s + 128], T.WT16[:], R=["ES%d" % s, "WT16"])
        for b in range(16):
            mm(P[6][:, b::16], T.XR[:, 144 * b + 1 - t:144 * b + 129 - t], T.HAS2[:], False, b == 15,
               R=["XR%d" % b, "HAS2"])
        mm(P[2][:], T.ID[:], own[:])
        tt(T.AB[:], T.AA[:], T.SELF16[:], A.add)
        cp(T.IDX[:], T.CI[:])
        tt(T.D1[:], T.AA[:], T.TX[:], A.add)
        tt(T.CL[:], T.WT16[:], T.AB[:], A.min)
        tt(T.DX[:], T.CX[:], T.SELF[:], A.subtract)
        ts(T.CU[:], T.CL[:], 2048.0, None, A.add)
        cp(T.WN2[:], P[4][:, 0:256])
        act(T.SA[:], T.W[:, 0:4096].indirect(T.CU[:, 0:32]), F.Copy, R=WK + ["CU"])
        act(T.ZH[:], P[6][:], F.Relu, bias=-2048.0)
        tt(T.EQ[:], T.WN2[:, 0:256].indirect(T.IDX[:, 0:32]), T.NR[:], A.is_equal, R=["WN2", "IDX", "NR"])
        mm(P[7][:], T.IM[:, 128 * t:128 * t + 128], t16[:], True, False, R=kt + ["IM%d" % t])
        for b in range(16):
            mm(P[0][:, 0:32], T.BL[:, 15 - b:143 - b], T.EQ[:, b::16], b == 0, b == 15)
        tt(T.NEW[:], T.D1[:], T.WT16[:], A.min)
        tt(T.NZ[:], T.SA[:], P[2][:], A.max, W=NZK)
        tt(T.E1[:], P[0][:, 0:32], T.DX[:], A.mult)
        tt(T.C2[:], T.E1[:], T.SELFK[:], A.add)
        ts(T.C2U[:], T.C2[:], 1.0 / 2048.0, None, A.mult)
        for b in range(16):
            mm(P[7][:, b::16], T.XR[:, 144 * b + 1 - t:144 * b + 129 - t], T.NEW[:], False, False,
               R=["XR%d" % b, "NEW"])
        if last:
            mm(P[7][:], T.R2K[0:1, :], T.ONES[0:1, :], False, False)
        mm(P[7][:], T.IDN[:], T.ZH[:], False, True)
        act(T.GT[:], T.TT[:, 0:4096].indirect(T.C2U[:, 0:32]), F.Identity, bias=2048.0 if last else 0.0,
            R=TTK + ["C2U"])
        tt(new[:], T.W[:, 0:4096].indirect(T.C2U[:, 0:32]), T.NZ[:], A.max, R=WK + NZK + ["C2U"])

        def low(k):
            c = half[k] if last else part[k]
            tt(T.EE[:, c], T.GT[:, c], P[6][:, c], A.min, W=["EE%d" % k])

        def numbers(out, k):
            c = half[k] if last else part[k]
            tt(out[:, c], T.EE[:, c], P[7][:, c], A.max, R=["EE%d" % k, "P7"], W=[nm(out[:]) + str(k)])

        low(0)
        low(1)
        if last:
            dma([("y", T.dS[:], new[:], [nm(new[:])], ["dS"])])
            dma([("s", T.oS[w], new[rows, :], [nm(new[:])], ["oSw"])])
            for k in range(2):
                numbers(T.TO, k)
                dma([("y", T["dT%d" % k][:], T.TO[:, half[k]], ["TO%d" % k], ["dT%d" % k])])
                dma([("s", T["oT%d" % k][w], T.TO[rows, half[k]], ["TO%d" % k], ["oTw%d" % k])])
            spread(T.dS, T.oS[w], "aS", ["dS"])
            for k in range(2):
                spread(T["dT%d" % k], T["oT%d" % k][w], "aT%d" % k, ["dT%d" % k])
        else:
            nxt = cores[(w + 1) % N]
            rid, pid, _se = topo.addr(nxt)
            for k in range(3):
                numbers(T.TN, k)
                if k == 0:
                    low(2)
                need("g", ["TN%d" % k], [])
                g.remote_dma(T.t1[:, part[k]], T.TN[:, part[k]], T.sem["ah%d" % k], T.sem.ls, pid, rid,
                             topo.mask(core, nxt))
                sent[0] += len(topo.engines(core, nxt))
                total["ah%d" % k] = len(topo.engines(cores[(w - 1) % N], core))
                wr["t1%d" % k] = ("ah%d" % k, total["ah%d" % k], "r")

    one_round(0)
    one_round(1)
    wr["oS"] = ("aS", N - 1, "r")
    dma([("s", T.ysec[:], T.oS[:], ["oS", "oSw"], ["ysec"])])
    for k in range(2):
        wr["oT%d" % k] = ("aT%d" % k, N - 1, "r")
        dma([("y", T.ytel[:, half[k]], T["oT%d" % k][:], ["oT%d" % k, "oTw%d" % k], ["ytel%d" % k])])
    total["ls"] = sent[0]
    total.update(cnt)
    for s, v in total.items():
        if seen["g"].get(s, 0) < v:
            g.wait_ge(T.sem[s], v)
